import numpy as np
import ml_dtypes


def mxq(x, axis, fmt="e4m3"):
    dtype, down = {"e4m3": (ml_dtypes.float8_e4m3fn, 7), "e5m2": (ml_dtypes.float8_e5m2, 14)}[fmt]
    v = np.moveaxis(np.asarray(x, np.float32).astype(ml_dtypes.bfloat16).astype(np.float64), axis, -1)
    blocks = v.reshape(v.shape[:-1] + (-1, 32))
    amax = np.abs(blocks).max(-1, keepdims=True)
    byte = np.maximum(np.where(amax > 0, np.frexp(amax)[1] - 1 + 127, 0) - down, 1)
    scale = np.exp2(byte - 127.0)
    codes = (blocks / scale).astype(np.float32).astype(dtype).astype(np.float64)
    return np.moveaxis((codes * scale).reshape(v.shape), -1, axis)


WIDE = False


def mx_kscale(k):
    if not WIDE:
        return np.ones(k)
    levels = np.array([24, -24, 12, -12, 0])
    if k % 512:
        return np.exp2(np.random.permutation(np.resize(levels, k // 32))).repeat(32)
    a = np.empty((k // 512, 16))
    for p in range(k // 512):
        a[p, :8] = np.random.permutation(np.resize(levels, 8))
        for g in range(8):
            far = levels[np.abs(levels - a[p, g]) >= 10]
            a[p, g + 8] = far[np.random.randint(len(far))]
    return np.exp2(a.ravel()).repeat(32)


def f64(x):
    return np.asarray(x).astype(np.float64)


def striped(idx):
    return np.tile(idx.reshape(-1, 16).T, (8, 1)).astype(np.uint16)


def unstriped(offs):
    return offs[:16].T.reshape(-1).astype(np.int64)


E2M1 = np.array([0.0, 0.5, 1.0, 1.5, 2.0, 3.0, 4.0, 6.0, -0.0, -0.5, -1.0, -1.5, -2.0, -3.0, -4.0, -6.0])


def pack_weight(w, fmt):
    k, n = w.shape
    w = f64(np.asarray(w, np.float32).astype(ml_dtypes.bfloat16)).reshape(k // 32, 32, n)
    amax = np.abs(w).max(1)
    if fmt == "e4m3":
        byte = np.frexp(amax)[1] - 1 + 127 - 7
    else:
        mant, ex = np.frexp(amax / 6.0)
        byte = np.where(mant > 0.5, ex, ex - 1) + 127
    byte = np.clip(np.where(amax > 0, byte, 1), 1, 254)
    scaled = (w * np.exp2(127.0 - byte)[:, None, :]).reshape(k, n).astype(np.float32)
    by_word = np.ascontiguousarray(scaled.reshape(k // 512, 128, 4, n).transpose(0, 1, 3, 2))
    if fmt == "e4m3":
        words = by_word.astype(ml_dtypes.float8_e4m3fn).view(np.uint8)
    else:
        c = by_word.astype(ml_dtypes.float4_e2m1fn).view(np.uint8) & 0xF
        words = (c[..., 0::2] | (c[..., 1::2] << 4)).reshape(k // 512, 128, 2 * n)
    return np.ascontiguousarray(words), np.ascontiguousarray(byte.astype(np.uint8).reshape(k // 512, 16, n))


def unpack_weight(words, scales, fmt):
    g, _, n = scales.shape
    words = np.ascontiguousarray(words).reshape(g, 128, n, -1)
    if fmt == "e4m3":
        vals = words.view(ml_dtypes.float8_e4m3fn).astype(np.float64)
    else:
        nib = np.empty((g, 128, n, 4), np.uint8)
        nib[..., 0::2] = words & 0xF
        nib[..., 1::2] = words >> 4
        vals = E2M1[nib]
    vals = vals * np.repeat(np.exp2(scales.astype(np.float64) - 127.0), 8, axis=1)[..., None]
    return vals.transpose(0, 1, 3, 2).reshape(g * 512, n)


def sigm(f):
    return 1.0 / (1.0 + np.exp(-np.maximum(f, -700.0)))


K, L, R, N, T, J = 512, 512, 1024, 512, 1024, 512


def setup_inputs():
    n = np.random.standard_normal
    s = mx_kscale(K)[:, None]
    s2 = mx_kscale(L)[:, None]
    u = mx_kscale(R)[:, None]
    en = n((R, N)) / np.sqrt(R) / u
    p_tab = pack_weight(n((K, T)) * s, "e4m3")
    p_tab2 = pack_weight(n((L, T)) * s2, "e4m3")
    p_wa = pack_weight(n((K, R)) / np.sqrt(K) / s * u.T, "e4m3")
    p_en8 = pack_weight(en[:512], "e4m3")
    p_en4 = pack_weight(en[512:], "e2m1")
    return {
        "tab_words": p_tab[0],
        "tab_scales": p_tab[1],
        "tab2_words": p_tab2[0],
        "tab2_scales": p_tab2[1],
        "wa_words": p_wa[0],
        "wa_scales": p_wa[1],
        "wb": (n((L, R)) / np.sqrt(L) / s2 * u.T).astype(np.float32),
        "en8_words": p_en8[0],
        "en8_scales": p_en8[1],
        "en4_words": p_en4[0],
        "en4_scales": p_en4[1],
        "offs": striped(np.random.permutation(T)[:J]),
        "offs2": striped(np.random.permutation(T)[:J]),
    }


def reference(tab_words, tab_scales, tab2_words, tab2_scales, wa_words, wa_scales, wb, en8_words, en8_scales, en4_words, en4_scales, offs, offs2):
    idx = unstriped(offs)
    idx2 = unstriped(offs2)
    tab_ = unpack_weight(tab_words, tab_scales, "e4m3")[:, idx]
    tab2_ = unpack_weight(tab2_words, tab2_scales, "e4m3")[:, idx2]
    wa_ = unpack_weight(wa_words, wa_scales, "e4m3")
    wb_ = mxq(f64(wb), 0, "e4m3")
    z = wa_.T @ tab_ + wb_.T @ tab2_
    h = np.maximum(z, 0.0)
    h_ = mxq(h, 0, "e4m3")
    en8_ = unpack_weight(en8_words, en8_scales, "e4m3")
    en4_ = unpack_weight(en4_words, en4_scales, "e2m1")
    y = en8_.T @ h_[:512] + en4_.T @ h_[512:]
    return sigm(y)

@@ -1,0 +1,203 @@
+from contextlib import ExitStack
+
+import concourse.mybir as mybir
+
+K, L, R, N, T, J = 512, 512, 1024, 512, 1024, 512
+FLOPS = 2 * (K + L) * R * J + 2 * R * N * J
+
+F32 = mybir.dt.float32
+BF16 = mybir.dt.bfloat16
+I32 = mybir.dt.int32
+U32 = mybir.dt.uint32
+U16 = mybir.dt.uint16
+U8 = mybir.dt.uint8
+FP8X4 = mybir.dt.float8_e4m3fn_x4
+FP4X4 = mybir.dt.float4_e2m1fn_x4
+ACT = mybir.ActivationFunctionType
+
+P = 128
+PACK = 4
+PASS = P * PACK
+HALVES = R // PASS
+CHUNK = 128
+CHUNKS = J // CHUNK
+QUARTER = PASS // 2
+QM = QUARTER // PACK
+NT = N // P
+
+TAB_ROW, TAB2_ROW = 12, 8
+WA_ROW = (0, 4)
+EN8_ROW, EN4_ROW = 4, 0
+
+
+def tile_list_kg_relu_mix_sig_kernel(
+    tc, tab_words, tab_scales, tab2_words, tab2_scales, wa_words, wa_scales, wb,
+    en8_words, en8_scales, en4_words, en4_scales, offs, offs2, out,
+):
+    nc = tc.nc
+    with ExitStack() as ctx:
+        sb = ctx.enter_context(tc.tile_pool(name="sb", bufs=1))
+        ps = ctx.enter_context(tc.psum_pool(name="ps", bufs=1))
+
+        def tile(name, shape, dtype):
+            return sb.tile(shape, dtype, name=name, align_bytes=64)
+
+        idx = tile("idx", [P, J // 16], U16)
+        idx2 = tile("idx2", [P, J // 16], U16)
+        tab_w = tile("tab_w", [P, T], I32)
+        tab_s = tile("tab_s", [P, T], U8)
+        tab2_w = tile("tab2_w", [P, T], I32)
+        tab2_s = tile("tab2_s", [P, T], U8)
+        wa_w = tile("wa_w", [P, R], I32)
+        wa_s = tile("wa_s", [P, PASS], U8)
+        en8_w = tile("en8_w", [P, N], I32)
+        en4_w = tile("en4_w", [P, 2 * N], U8)
+        en_s = tile("en_s", [P, N], U8)
+        wb_raw = [tile("wb_raw%d" % q, [P, PACK, QUARTER], F32) for q in range(R // QUARTER)]
+        warm_in = tile("warm_in", [P, 1], F32)
+        warm_out = tile("warm_out", [P, 1], F32)
+
+        for plane in (tab_s, wa_s, tab2_s, en_s):
+            nc.vector.memset(plane[:].bitcast(I32), 0)
+        nc.vector.memset(warm_in[:], 0.0)
+        nc.scalar.activation(warm_out[:], warm_in[:], ACT.Sigmoid)
+
+        def load_words(dst, src):
+            nc.sync.dma_start(dst[:], src[0].rearrange("p n i -> p (n i)").bitcast(I32))
+
+        def load_scales(dst, row, src, eng):
+            for quad in range(4):
+                first = 32 * quad + row
+                eng.dma_start(dst[first : first + 4, :].bitcast(I32), src[0, 4 * quad : 4 * quad + 4, :].bitcast(I32))
+
+        def load_wb(q):
+            rows = wb.rearrange("(p i) r -> p i r", i=PACK)
+            nc.sync.dma_start(wb_raw[q][:], rows[:, :, q * QUARTER : (q + 1) * QUARTER])
+
+        nc.sync.dma_start(idx[:], offs)
+        load_words(tab_w, tab_words)
+        load_words(wa_w, wa_words)
+        load_scales(tab_s, TAB_ROW, tab_scales, nc.sync)
+        load_wb(0)
+        for quad in range(4):
+            src = wa_scales[0, 4 * quad : 4 * quad + 4, :].bitcast(I32).rearrange("r (b n) -> b r n", b=HALVES)
+            nc.sync.dma_start(wa_s[32 * quad : 32 * quad + 8, :].bitcast(I32), src)
+        nc.sync.dma_start(idx2[:], offs2)
+        load_words(tab2_w, tab2_words)
+        load_scales(tab2_s, TAB2_ROW, tab2_scales, nc.sync)
+        for q in (1, 2, 3):
+            load_wb(q)
+        load_scales(en_s, EN8_ROW, en8_scales, nc.sync)
+        load_words(en8_w, en8_words)
+        load_scales(en_s, EN4_ROW, en4_scales, nc.sync)
+        nc.sync.dma_start(en4_w[:].bitcast(I32), en4_words[0].bitcast(I32))
+
+        v_w = tile("v_w", [P, J], U32)
+        v_s = tile("v_s", [P, J], U8)
+        v2_w = tile("v2_w", [P, J], U32)
+        v2_s = tile("v2_s", [P, J], U8)
+        wa_pw = [tile("wa_pw%d" % b, [P, PASS], I32) for b in range(HALVES)]
+        wa_ps = tile("wa_ps", [P, PASS], U8)
+        wb_bf = [tile("wb_bf%d" % q, [P, PACK, QM, PACK], BF16) for q in range(R // QUARTER)]
+        wb_w = [tile("wb_w%d" % b, [P, PASS], U32) for b in range(HALVES)]
+        wb_s = [tile("wb_s%d" % b, [P, PASS], U8) for b in range(HALVES)]
+        h_bf = [[tile("h_bf%d_%d" % (b, c), [P, CHUNK, PACK], BF16) for c in range(CHUNKS)] for b in range(HALVES)]
+        h_w = [[tile("h_w%d_%d" % (b, c), [P, CHUNK], U32) for c in range(CHUNKS)] for b in range(HALVES)]
+        h_s = [[tile("h_s%d_%d" % (b, c), [P, CHUNK], U8) for c in range(CHUNKS)] for b in range(HALVES)]
+        z = [[ps.tile([P, PACK, CHUNK], F32, name="z%d_%d" % (b, c), tag="bank%d_%d" % (b, c)) for c in range(CHUNKS)] for b in range(HALVES)]
+
+        def deal_wa_words(b):
+            nc.vector.tensor_copy(
+                wa_pw[b][:].rearrange("p (t g m) -> p g t m", t=PACK, m=4),
+                wa_w[:, b * PASS : (b + 1) * PASS].rearrange("p (g m t) -> p g t m", t=PACK, m=4),
+            )
+
+        def round_wb(q, copy):
+            copy(wb_bf[q][:].rearrange("p t m i -> p m i t"), wb_raw[q][:].rearrange("p i (m t) -> p m i t", t=PACK))
+
+        def quantise_wb(q):
+            b, half = divmod(q, 2)
+            for t in range(PACK):
+                cols = slice(t * P + half * QM, t * P + (half + 1) * QM)
+                nc.vector.quantize_mx(
+                    out=wb_w[b][:, cols].bitcast(FP8X4), scales=wb_s[b][:, cols],
+                    in_=wb_bf[q][:, t].rearrange("p m i -> p (m i)"),
+                )
+
+        def wa_passes(b):
+            for c in range(CHUNKS):
+                js = slice(c * CHUNK, (c + 1) * CHUNK)
+                for t in range(PACK):
+                    cols = slice(t * P, (t + 1) * P)
+                    nc.tensor.matmul_mx(
+                        out=z[b][c][:, t, :], lhsT=wa_pw[b][:, cols].bitcast(FP8X4), lhsT_scale=wa_ps[WA_ROW[b] :, cols],
+                        rhs=v_w[:, js].bitcast(FP8X4), rhs_scale=v_s[TAB_ROW:, js], start=(t == 0), stop=False,
+                    )
+
+        def wb_passes(b, c):
+            js = slice(c * CHUNK, (c + 1) * CHUNK)
+            for t in range(PACK):
+                cols = slice(t * P, (t + 1) * P)
+                nc.tensor.matmul_mx(
+                    out=z[b][c][:, t, :], lhsT=wb_w[b][:, cols].bitcast(FP8X4), lhsT_scale=wb_s[b][:, cols],
+                    rhs=v2_w[:, js].bitcast(FP8X4), rhs_scale=v2_s[TAB2_ROW:, js], start=False, stop=(t == PACK - 1),
+                )
+
+        def relu(b, c, on_scalar):
+            src = z[b][c][:].rearrange("p t j -> p j t")
+            if on_scalar:
+                nc.scalar.activation(h_bf[b][c][:], src, ACT.Relu)
+            else:
+                nc.vector.tensor_scalar_max(h_bf[b][c][:], src, 0.0)
+
+        def quantise_h(b, c):
+            nc.vector.quantize_mx(
+                out=h_w[b][c][:].bitcast(FP8X4), scales=h_s[b][c][:], in_=h_bf[b][c][:].rearrange("p j t -> p (j t)"),
+            )
+
+        nc.vector.tensor_copy(v_w[:], tab_w[:].bitcast(U32).indirect(idx[:]))
+        deal_wa_words(0)
+        nc.vector.tensor_copy(v_s[:], tab_s[:].indirect(idx[:]))
+        nc.vector.tensor_copy(wa_ps[:].rearrange("p (t m) -> p t m", t=PACK), wa_s[:].rearrange("p (m t) -> p t m", t=PACK))
+        wa_passes(0)
+        deal_wa_words(1)
+        wa_passes(1)
+        round_wb(0, nc.scalar.copy)
+        nc.vector.tensor_copy(v2_s[:], tab2_s[:].indirect(idx2[:]))
+        nc.vector.tensor_copy(v2_w[:], tab2_w[:].bitcast(U32).indirect(idx2[:]))
+        quantise_wb(0)
+        round_wb(1, nc.scalar.copy)
+        quantise_wb(1)
+        for c in range(CHUNKS):
+            wb_passes(0, c)
+        round_wb(2, nc.scalar.copy)
+        quantise_wb(2)
+        round_wb(3, nc.vector.tensor_copy)
+        quantise_wb(3)
+        for c in range(CHUNKS):
+            wb_passes(1, c)
+        for c in range(CHUNKS):
+            relu(0, c, on_scalar=(c != 3))
+            quantise_h(0, c)
+        y = [ps.tile([P, NT, CHUNK], F32, name="y%d" % c, tag="bank0_%d" % c) for c in range(CHUNKS)]
+        for c in range(CHUNKS):
+            for nt in range(NT):
+                cols = slice(nt * P, (nt + 1) * P)
+                nc.tensor.matmul_mx(
+                    out=y[c][:, nt, :], lhsT=en8_w[:, cols].bitcast(FP8X4), lhsT_scale=en_s[EN8_ROW:, cols],
+                    rhs=h_w[0][c][:].bitcast(FP8X4), rhs_scale=h_s[0][c][:], start=(nt == 0), stop=False,
+                )
+        for c in range(CHUNKS):
+            relu(1, c, on_scalar=(c % 2 == 0))
+        out_rows = out.rearrange("(nt p) j -> p nt j", p=P)
+        for c in range(CHUNKS):
+            quantise_h(1, c)
+            for nt in range(NT):
+                nc.tensor.matmul_mx(
+                    out=y[c][:, nt, :], lhsT=en4_w[:, 2 * nt * P : 2 * (nt + 1) * P].bitcast(FP4X4),
+                    lhsT_scale=en_s[EN4_ROW:, nt * P : (nt + 1) * P],
+                    rhs=h_w[1][c][:].bitcast(FP8X4), rhs_scale=h_s[1][c][:], start=False, stop=(nt == NT - 1),
+                )
+            res = tile("res%d" % c, [P, NT, CHUNK], F32)
+            nc.scalar.activation(res[:], y[c][:], ACT.Sigmoid)
+            nc.sync.dma_start(out_rows[:, :, c * CHUNK : (c + 1) * CHUNK], res[:])

@@ -24,6 +24,7 @@ CHUNKS = J // CHUNK
 QUARTER = PASS // 2
 QM = QUARTER // PACK
 NT = N // P
+JH = J // 2
 
 TAB_ROW, TAB2_ROW = 12, 8
 WA_ROW = (0, 4)
@@ -39,8 +40,8 @@ def tile_list_kg_relu_mix_sig_kernel(
         sb = ctx.enter_context(tc.tile_pool(name="sb", bufs=1))
         ps = ctx.enter_context(tc.psum_pool(name="ps", bufs=1))
 
-        def tile(name, shape, dtype):
-            return sb.tile(shape, dtype, name=name, align_bytes=64)
+        def tile(name, shape, dtype, slot=None):
+            return sb.tile(shape, dtype, name=name, tag=slot or name, align_bytes=64)
 
         idx = tile("idx", [P, J // 16], U16)
         idx2 = tile("idx2", [P, J // 16], U16)
@@ -53,7 +54,8 @@ def tile_list_kg_relu_mix_sig_kernel(
         en8_w = tile("en8_w", [P, N], I32)
         en4_w = tile("en4_w", [P, 2 * N], U8)
         en_s = tile("en_s", [P, N], U8)
-        wb_raw = [tile("wb_raw%d" % q, [P, PACK, QUARTER], F32) for q in range(R // QUARTER)]
+        wb_raw0 = tile("wb_raw0", [P, PACK, PASS], F32)
+        wb_raw1 = [tile("wb_raw1_%d" % q, [P, PACK, QUARTER], F32) for q in range(2)]
         warm_in = tile("warm_in", [P, 1], F32)
         warm_out = tile("warm_out", [P, 1], F32)
 
@@ -66,44 +68,43 @@ def tile_list_kg_relu_mix_sig_kernel(
             nc.sync.dma_start(dst[:], src[0].rearrange("p n i -> p (n i)").bitcast(I32))
 
         def load_scales(dst, row, src, eng):
-            for quad in range(4):
-                first = 32 * quad + row
-                eng.dma_start(dst[first : first + 4, :].bitcast(I32), src[0, 4 * quad : 4 * quad + 4, :].bitcast(I32))
+            for r in range(4):
+                eng.dma_start(dst[row + r : P : 32, :].bitcast(I32), src[0, r:16:4, :].bitcast(I32))
 
-        def load_wb(q):
+        def load_wb(dst, first, width):
             rows = wb.rearrange("(p i) r -> p i r", i=PACK)
-            nc.sync.dma_start(wb_raw[q][:], rows[:, :, q * QUARTER : (q + 1) * QUARTER])
+            nc.sync.dma_start(dst[:], rows[:, :, first : first + width])
+
+        def load_wa_scales(quad, eng):
+            src = wa_scales[0, 4 * quad : 4 * quad + 4, :].bitcast(I32).rearrange("r (b n) -> b r n", b=HALVES)
+            eng.dma_start(wa_s[32 * quad : 32 * quad + 8, :].bitcast(I32), src)
 
         nc.sync.dma_start(idx[:], offs)
         load_words(tab_w, tab_words)
-        load_words(wa_w, wa_words)
         load_scales(tab_s, TAB_ROW, tab_scales, nc.sync)
-        load_wb(0)
-        for quad in range(4):
-            src = wa_scales[0, 4 * quad : 4 * quad + 4, :].bitcast(I32).rearrange("r (b n) -> b r n", b=HALVES)
-            nc.sync.dma_start(wa_s[32 * quad : 32 * quad + 8, :].bitcast(I32), src)
-        nc.sync.dma_start(idx2[:], offs2)
+        load_words(wa_w, wa_words)
         load_words(tab2_w, tab2_words)
+        for quad in range(4):
+            load_wa_scales(quad, nc.sync)
+        nc.sync.dma_start(idx2[:], offs2)
+        load_wb(wb_raw0, 0, PASS)
         load_scales(tab2_s, TAB2_ROW, tab2_scales, nc.sync)
-        for q in (1, 2, 3):
-            load_wb(q)
+        for q in range(2):
+            load_wb(wb_raw1[q], PASS + q * QUARTER, QUARTER)
         load_scales(en_s, EN8_ROW, en8_scales, nc.sync)
         load_words(en8_w, en8_words)
-        load_scales(en_s, EN4_ROW, en4_scales, nc.sync)
         nc.sync.dma_start(en4_w[:].bitcast(I32), en4_words[0].bitcast(I32))
+        load_scales(en_s, EN4_ROW, en4_scales, nc.sync)
 
         v_w = tile("v_w", [P, J], U32)
         v_s = tile("v_s", [P, J], U8)
         v2_w = tile("v2_w", [P, J], U32)
         v2_s = tile("v2_s", [P, J], U8)
-        wa_pw = [tile("wa_pw%d" % b, [P, PASS], I32) for b in range(HALVES)]
+        wa_pw = [tile("wa_pw0", [P, PASS], I32)]
         wa_ps = tile("wa_ps", [P, PASS], U8)
-        wb_bf = [tile("wb_bf%d" % q, [P, PACK, QM, PACK], BF16) for q in range(R // QUARTER)]
+        wb_bf = [tile("wb_bf%d" % b, [P, PACK, P, PACK], BF16) for b in range(HALVES)]
         wb_w = [tile("wb_w%d" % b, [P, PASS], U32) for b in range(HALVES)]
-        wb_s = [tile("wb_s%d" % b, [P, PASS], U8) for b in range(HALVES)]
-        h_bf = [[tile("h_bf%d_%d" % (b, c), [P, CHUNK, PACK], BF16) for c in range(CHUNKS)] for b in range(HALVES)]
-        h_w = [[tile("h_w%d_%d" % (b, c), [P, CHUNK], U32) for c in range(CHUNKS)] for b in range(HALVES)]
-        h_s = [[tile("h_s%d_%d" % (b, c), [P, CHUNK], U8) for c in range(CHUNKS)] for b in range(HALVES)]
+        h_s = [tile("h_s%d" % b, [P, J], U8) for b in range(HALVES)]
         z = [[ps.tile([P, PACK, CHUNK], F32, name="z%d_%d" % (b, c), tag="bank%d_%d" % (b, c)) for c in range(CHUNKS)] for b in range(HALVES)]
 
         def deal_wa_words(b):
@@ -112,92 +113,90 @@ def tile_list_kg_relu_mix_sig_kernel(
                 wa_w[:, b * PASS : (b + 1) * PASS].rearrange("p (g m t) -> p g t m", t=PACK, m=4),
             )
 
-        def round_wb(q, copy):
-            copy(wb_bf[q][:].rearrange("p t m i -> p m i t"), wb_raw[q][:].rearrange("p i (m t) -> p m i t", t=PACK))
+        def round_wb(dst, raw, copy):
+            copy(dst.rearrange("p t m i -> p m i t"), raw.rearrange("p i m t -> p m i t"))
 
-        def quantise_wb(q):
-            b, half = divmod(q, 2)
-            for t in range(PACK):
-                cols = slice(t * P + half * QM, t * P + (half + 1) * QM)
-                nc.vector.quantize_mx(
-                    out=wb_w[b][:, cols].bitcast(FP8X4), scales=wb_s[b][:, cols],
-                    in_=wb_bf[q][:, t].rearrange("p m i -> p (m i)"),
-                )
+        def quantise(words, scales, values):
+            nc.vector.quantize_mx(out=words.bitcast(FP8X4), scales=scales, in_=values)
 
-        def wa_passes(b):
-            for c in range(CHUNKS):
-                js = slice(c * CHUNK, (c + 1) * CHUNK)
-                for t in range(PACK):
-                    cols = slice(t * P, (t + 1) * P)
-                    nc.tensor.matmul_mx(
-                        out=z[b][c][:, t, :], lhsT=wa_pw[b][:, cols].bitcast(FP8X4), lhsT_scale=wa_ps[WA_ROW[b] :, cols],
-                        rhs=v_w[:, js].bitcast(FP8X4), rhs_scale=v_s[TAB_ROW:, js], start=(t == 0), stop=False,
-                    )
+        def quantise_wb(b):
+            for t in (0, 2):
+                cols = slice(t * P, (t + 2) * P)
+                quantise(wb_w[b][:, cols], wb_s[b][:, cols], wb_bf[b][:, t : t + 2].rearrange("p t m i -> p (t m i)"))
 
-        def wb_passes(b, c):
-            js = slice(c * CHUNK, (c + 1) * CHUNK)
+        def z_passes(b, c, lhs_w, lhs_s, rhs_w, rhs_s, first):
             for t in range(PACK):
                 cols = slice(t * P, (t + 1) * P)
                 nc.tensor.matmul_mx(
-                    out=z[b][c][:, t, :], lhsT=wb_w[b][:, cols].bitcast(FP8X4), lhsT_scale=wb_s[b][:, cols],
-                    rhs=v2_w[:, js].bitcast(FP8X4), rhs_scale=v2_s[TAB2_ROW:, js], start=False, stop=(t == PACK - 1),
+                    out=z[b][c][:, t, :], lhsT=lhs_w[:, cols].bitcast(FP8X4), lhsT_scale=lhs_s[:, cols],
+                    rhs=rhs_w.bitcast(FP8X4), rhs_scale=rhs_s,
+                    start=(first and t == 0), stop=(not first and t == PACK - 1),
                 )
 
-        def relu(b, c, on_scalar):
+        def relu(dst, b, c, on_scalar):
             src = z[b][c][:].rearrange("p t j -> p j t")
             if on_scalar:
-                nc.scalar.activation(h_bf[b][c][:], src, ACT.Relu)
+                nc.scalar.activation(dst, src, ACT.Relu)
             else:
-                nc.vector.tensor_scalar_max(h_bf[b][c][:], src, 0.0)
-
-        def quantise_h(b, c):
-            nc.vector.quantize_mx(
-                out=h_w[b][c][:].bitcast(FP8X4), scales=h_s[b][c][:], in_=h_bf[b][c][:].rearrange("p j t -> p (j t)"),
-            )
+                nc.vector.tensor_scalar_max(dst, src, 0.0)
 
         nc.vector.tensor_copy(v_w[:], tab_w[:].bitcast(U32).indirect(idx[:]))
-        deal_wa_words(0)
         nc.vector.tensor_copy(v_s[:], tab_s[:].indirect(idx[:]))
+        deal_wa_words(0)
         nc.vector.tensor_copy(wa_ps[:].rearrange("p (t m) -> p t m", t=PACK), wa_s[:].rearrange("p (m t) -> p t m", t=PACK))
-        wa_passes(0)
+        wa_pw.append(tile("wa_pw1", [P, PASS], I32, slot="wa_s"))
         deal_wa_words(1)
-        wa_passes(1)
-        round_wb(0, nc.scalar.copy)
-        nc.vector.tensor_copy(v2_s[:], tab2_s[:].indirect(idx2[:]))
         nc.vector.tensor_copy(v2_w[:], tab2_w[:].bitcast(U32).indirect(idx2[:]))
+        raw0 = wb_raw0[:].rearrange("p i (m t) -> p i m t", t=PACK)
+        raw1 = [raw[:].rearrange("p i (m t) -> p i m t", t=PACK) for raw in wb_raw1]
+        round_wb(wb_bf[0][:, 0:2], raw0[:, :, :, 0:2], nc.vector.tensor_copy)
+        round_wb(wb_bf[0][:, 2:4], raw0[:, :, :, 2:4], nc.scalar.copy)
+        round_wb(wb_bf[1][:, :, 0:QM], raw1[0], nc.scalar.copy)
+        nc.vector.tensor_copy(v2_s[:], tab2_s[:].indirect(idx2[:]))
+        wb_s = [tile("wb_s0", [P, PASS], U8, slot="tab2_s"), tile("wb_s1", [P, PASS], U8)]
         quantise_wb(0)
-        round_wb(1, nc.scalar.copy)
+        round_wb(wb_bf[1][:, :, QM:P], raw1[1], nc.vector.tensor_copy)
         quantise_wb(1)
+        for b in range(HALVES):
+            for c in range(CHUNKS):
+                js = slice(c * CHUNK, (c + 1) * CHUNK)
+                z_passes(b, c, wa_pw[b][:], wa_ps[WA_ROW[b] :, :], v_w[:, js], v_s[TAB_ROW:, js], first=True)
+            for c in range(CHUNKS):
+                js = slice(c * CHUNK, (c + 1) * CHUNK)
+                z_passes(b, c, wb_w[b][:], wb_s[b][:], v2_w[:, js], v2_s[TAB2_ROW:, js], first=False)
+
+        h_bf0 = [tile("h_bf0_%d" % jh, [P, JH, PACK], BF16, slot=slot) for jh, slot in enumerate(("wb_raw1_0", "wb_raw1_1"))]
+        h_w0 = tile("h_w0", [P, J], U32, slot="wb_bf1")
+        h_bf1 = tile("h_bf1", [P, J, PACK], BF16)
+        h_w1 = tile("h_w1", [P, J], U32)
         for c in range(CHUNKS):
-            wb_passes(0, c)
-        round_wb(2, nc.scalar.copy)
-        quantise_wb(2)
-        round_wb(3, nc.vector.tensor_copy)
-        quantise_wb(3)
-        for c in range(CHUNKS):
-            wb_passes(1, c)
-        for c in range(CHUNKS):
-            relu(0, c, on_scalar=(c != 3))
-            quantise_h(0, c)
-        y = [ps.tile([P, NT, CHUNK], F32, name="y%d" % c, tag="bank0_%d" % c) for c in range(CHUNKS)]
-        for c in range(CHUNKS):
+            relu(h_bf0[c // 2][:, c % 2 * CHUNK : (c % 2 + 1) * CHUNK, :], 0, c, on_scalar=(c != 3))
+
+        out_rows = out.rearrange("(nt p) j -> p nt j", p=P)
+        for jh in range(2):
+            half = slice(jh * JH, (jh + 1) * JH)
+            for c in (2 * jh, 2 * jh + 1):
+                relu(h_bf1[:, c * CHUNK : (c + 1) * CHUNK, :], 1, c, on_scalar=(c != 1))
+            quantise(h_w0[:, half], h_s[0][:, half], h_bf0[jh][:].rearrange("p j t -> p (j t)"))
+            y = [ps.tile([P, 2, JH], F32, name="y%d_%d" % (jh, pair), tag="bank0_%d" % (2 * jh + pair)) for pair in range(2)]
             for nt in range(NT):
                 cols = slice(nt * P, (nt + 1) * P)
                 nc.tensor.matmul_mx(
-                    out=y[c][:, nt, :], lhsT=en8_w[:, cols].bitcast(FP8X4), lhsT_scale=en_s[EN8_ROW:, cols],
-                    rhs=h_w[0][c][:].bitcast(FP8X4), rhs_scale=h_s[0][c][:], start=(nt == 0), stop=False,
+                    out=y[nt // 2][:, nt % 2, :], lhsT=en8_w[:, cols].bitcast(FP8X4), lhsT_scale=en_s[EN8_ROW:, cols],
+                    rhs=h_w0[:, half].bitcast(FP8X4), rhs_scale=h_s[0][:, half], start=(nt % 2 == 0), stop=False,
                 )
-        for c in range(CHUNKS):
-            relu(1, c, on_scalar=(c % 2 == 0))
-        out_rows = out.rearrange("(nt p) j -> p nt j", p=P)
-        for c in range(CHUNKS):
-            quantise_h(1, c)
-            for nt in range(NT):
-                nc.tensor.matmul_mx(
-                    out=y[c][:, nt, :], lhsT=en4_w[:, 2 * nt * P : 2 * (nt + 1) * P].bitcast(FP4X4),
-                    lhsT_scale=en_s[EN4_ROW:, nt * P : (nt + 1) * P],
-                    rhs=h_w[1][c][:].bitcast(FP8X4), rhs_scale=h_s[1][c][:], start=False, stop=(nt == NT - 1),
-                )
-            res = tile("res%d" % c, [P, NT, CHUNK], F32)
-            nc.scalar.activation(res[:], y[c][:], ACT.Sigmoid)
-            nc.sync.dma_start(out_rows[:, :, c * CHUNK : (c + 1) * CHUNK], res[:])
+            quantise(h_w1[:, half], h_s[1][:, half], h_bf1[:, half, :].rearrange("p j t -> p (j t)"))
+            for pair in range(2):
+                for c in (2 * jh, 2 * jh + 1):
+                    js = slice(c * CHUNK, (c + 1) * CHUNK)
+                    for nt in (2 * pair, 2 * pair + 1):
+                        nc.tensor.matmul_mx(
+                            out=y[pair][:, nt % 2, c % 2 * CHUNK : (c % 2 + 1) * CHUNK],
+                            lhsT=en4_w[:, 2 * nt * P : 2 * (nt + 1) * P].bitcast(FP4X4),
+                            lhsT_scale=en_s[EN4_ROW:, nt * P : (nt + 1) * P],
+                            rhs=h_w1[:, js].bitcast(FP8X4), rhs_scale=h_s[1][:, js],
+                            start=False, stop=(c % 2 == 1 and nt % 2 == 1),
+                        )
+                res = tile("res%d_%d" % (jh, pair), [P, 2, JH], F32)
+                nc.scalar.activation(res[:], y[pair][:], ACT.Sigmoid)
+                nc.sync.dma_start(out_rows[:, 2 * pair : 2 * pair + 2, half], res[:])

@@ -79,8 +79,8 @@ def tile_list_kg_relu_mix_sig_kernel(
             src = wa_scales[0, 4 * quad : 4 * quad + 4, :].bitcast(I32).rearrange("r (b n) -> b r n", b=HALVES)
             eng.dma_start(wa_s[32 * quad : 32 * quad + 8, :].bitcast(I32), src)
 
-        nc.sync.dma_start(idx[:], offs)
         load_words(tab_w, tab_words)
+        nc.sync.dma_start(idx[:], offs)
         load_scales(tab_s, TAB_ROW, tab_scales, nc.sync)
         load_words(wa_w, wa_words)
         load_words(tab2_w, tab2_words)
@@ -155,7 +155,8 @@ def tile_list_kg_relu_mix_sig_kernel(
         nc.vector.tensor_copy(v2_s[:], tab2_s[:].indirect(idx2[:]))
         wb_s = [tile("wb_s0", [P, PASS], U8, slot="tab2_s"), tile("wb_s1", [P, PASS], U8)]
         quantise_wb(0)
-        round_wb(wb_bf[1][:, :, QM:P], raw1[1], nc.vector.tensor_copy)
+        for t in (0, 2):
+            round_wb(wb_bf[1][:, t : t + 2, QM:P], raw1[1][:, :, :, t : t + 2], nc.vector.tensor_copy)
         quantise_wb(1)
         for b in range(HALVES):
             for c in range(CHUNKS):
@@ -198,5 +199,8 @@ def tile_list_kg_relu_mix_sig_kernel(
                             start=False, stop=(c % 2 == 1 and nt % 2 == 1),
                         )
                 res = tile("res%d_%d" % (jh, pair), [P, 2, JH], F32)
-                nc.scalar.activation(res[:], y[pair][:], ACT.Sigmoid)
-                nc.sync.dma_start(out_rows[:, 2 * pair : 2 * pair + 2, half], res[:])
+                last = jh == 1 and pair == 1
+                for first, count in ((0, 1), (1, 1)) if last else ((0, 2),):
+                    part = slice(first, first + count)
+                    nc.scalar.activation(res[:, part], y[pair][:, part], ACT.Sigmoid)
+                    nc.sync.dma_start(out_rows[:, 2 * pair + first : 2 * pair + first + count, half], res[:, part])

@@ -29,6 +29,10 @@ JH = J // 2
 TAB_ROW, TAB2_ROW = 12, 8
 WA_ROW = (0, 4)
 EN8_ROW, EN4_ROW = 4, 0
+Y_GROUPS = (
+    (("bank0_0", (0,)), ("bank0_1", (1,)), ("bank0_2", (2, 3))),
+    (("bank0_3", (0, 1)), ("bank1_0", (2, 3))),
+)
 
 
 def tile_list_kg_relu_mix_sig_kernel(
@@ -91,10 +95,10 @@ def tile_list_kg_relu_mix_sig_kernel(
         load_scales(tab2_s, TAB2_ROW, tab2_scales, nc.sync)
         for q in range(2):
             load_wb(wb_raw1[q], PASS + q * QUARTER, QUARTER)
-        load_scales(en_s, EN8_ROW, en8_scales, nc.sync)
-        load_words(en8_w, en8_words)
         nc.sync.dma_start(en4_w[:].bitcast(I32), en4_words[0].bitcast(I32))
         load_scales(en_s, EN4_ROW, en4_scales, nc.sync)
+        load_words(en8_w, en8_words)
+        load_scales(en_s, EN8_ROW, en8_scales, nc.sync)
 
         v_w = tile("v_w", [P, J], U32)
         v_s = tile("v_s", [P, J], U8)
@@ -179,28 +183,30 @@ def tile_list_kg_relu_mix_sig_kernel(
             for c in (2 * jh, 2 * jh + 1):
                 relu(h_bf1[:, c * CHUNK : (c + 1) * CHUNK, :], 1, c, on_scalar=(c != 1))
             quantise(h_w0[:, half], h_s[0][:, half], h_bf0[jh][:].rearrange("p j t -> p (j t)"))
-            y = [ps.tile([P, 2, JH], F32, name="y%d_%d" % (jh, pair), tag="bank0_%d" % (2 * jh + pair)) for pair in range(2)]
-            for nt in range(NT):
-                cols = slice(nt * P, (nt + 1) * P)
-                nc.tensor.matmul_mx(
-                    out=y[nt // 2][:, nt % 2, :], lhsT=en8_w[:, cols].bitcast(FP8X4), lhsT_scale=en_s[EN8_ROW:, cols],
-                    rhs=h_w0[:, half].bitcast(FP8X4), rhs_scale=h_s[0][:, half], start=(nt % 2 == 0), stop=False,
-                )
+            groups = Y_GROUPS[jh]
+            y = [ps.tile([P, len(nts), JH], F32, name="y%d_%d" % (jh, nts[0]), tag=bank) for bank, nts in groups]
+            for g, (bank, nts) in enumerate(groups):
+                for place, nt in enumerate(nts):
+                    cols = slice(nt * P, (nt + 1) * P)
+                    nc.tensor.matmul_mx(
+                        out=y[g][:, place, :], lhsT=en8_w[:, cols].bitcast(FP8X4), lhsT_scale=en_s[EN8_ROW:, cols],
+                        rhs=h_w0[:, half].bitcast(FP8X4), rhs_scale=h_s[0][:, half], start=(place == 0), stop=False,
+                    )
             quantise(h_w1[:, half], h_s[1][:, half], h_bf1[:, half, :].rearrange("p j t -> p (j t)"))
-            for pair in range(2):
+            for g, (bank, nts) in enumerate(groups):
                 for c in (2 * jh, 2 * jh + 1):
                     js = slice(c * CHUNK, (c + 1) * CHUNK)
-                    for nt in (2 * pair, 2 * pair + 1):
+                    for place, nt in enumerate(nts):
                         nc.tensor.matmul_mx(
-                            out=y[pair][:, nt % 2, c % 2 * CHUNK : (c % 2 + 1) * CHUNK],
+                            out=y[g][:, place, c % 2 * CHUNK : (c % 2 + 1) * CHUNK],
                             lhsT=en4_w[:, 2 * nt * P : 2 * (nt + 1) * P].bitcast(FP4X4),
                             lhsT_scale=en_s[EN4_ROW:, nt * P : (nt + 1) * P],
                             rhs=h_w1[:, js].bitcast(FP8X4), rhs_scale=h_s[1][:, js],
-                            start=False, stop=(c % 2 == 1 and nt % 2 == 1),
+                            start=False, stop=(c % 2 == 1 and place == len(nts) - 1),
                         )
-                res = tile("res%d_%d" % (jh, pair), [P, 2, JH], F32)
-                last = jh == 1 and pair == 1
-                for first, count in ((0, 1), (1, 1)) if last else ((0, 2),):
+                res = tile("res%d_%d" % (jh, nts[0]), [P, len(nts), JH], F32)
+                last = jh == 1 and g == len(groups) - 1
+                for first, count in ((0, 1), (1, 1)) if last else ((0, len(nts)),):
                     part = slice(first, first + count)
-                    nc.scalar.activation(res[:, part], y[pair][:, part], ACT.Sigmoid)
-                    nc.sync.dma_start(out_rows[:, 2 * pair + first : 2 * pair + first + count, half], res[:, part])
+                    nc.scalar.activation(res[:, part], y[g][:, part], ACT.Sigmoid)
+                    nc.sync.dma_start(out_rows[:, nts[0] + first : nts[0] + first + count, half], res[:, part])

@@ -171,8 +171,7 @@ def tile_list_kg_relu_mix_sig_kernel(
                 z_passes(b, c, wb_w[b][:], wb_s[b][:], v2_w[:, js], v2_s[TAB2_ROW:, js], first=False)
 
         h_bf0 = [tile("h_bf0_%d" % jh, [P, JH, PACK], BF16, slot=slot) for jh, slot in enumerate(("wb_raw1_0", "wb_raw1_1"))]
-        h_w0 = tile("h_w0", [P, J], U32, slot="wb_bf1")
-        h_bf1 = tile("h_bf1", [P, J, PACK], BF16)
+        h_bf1 = [tile("h_bf1_%d" % c, [P, CHUNK, PACK], BF16) for c in range(CHUNKS)]
         h_w1 = tile("h_w1", [P, J], U32)
         for c in range(CHUNKS):
             relu(h_bf0[c // 2][:, c % 2 * CHUNK : (c % 2 + 1) * CHUNK, :], 0, c, on_scalar=(c != 3))
@@ -181,19 +180,29 @@ def tile_list_kg_relu_mix_sig_kernel(
         for jh in range(2):
             half = slice(jh * JH, (jh + 1) * JH)
             for c in (2 * jh, 2 * jh + 1):
-                relu(h_bf1[:, c * CHUNK : (c + 1) * CHUNK, :], 1, c, on_scalar=(c != 1))
-            quantise(h_w0[:, half], h_s[0][:, half], h_bf0[jh][:].rearrange("p j t -> p (j t)"))
+                relu(h_bf1[c][:], 1, c, on_scalar=(c != 1))
+            h_w0 = tile("h_w0_%d" % jh, [P, JH], U32, slot=("wb_bf1", "h_bf1_1")[jh])
+            quantise(h_w0[:], h_s[0][:, half], h_bf0[jh][:].rearrange("p j t -> p (j t)"))
             groups = Y_GROUPS[jh]
             y = [ps.tile([P, len(nts), JH], F32, name="y%d_%d" % (jh, nts[0]), tag=bank) for bank, nts in groups]
-            for g, (bank, nts) in enumerate(groups):
-                for place, nt in enumerate(nts):
+            for c in (2 * jh, 2 * jh + 1):
+                js = slice(c * CHUNK, (c + 1) * CHUNK)
+                quantise(h_w1[:, js], h_s[1][:, js], h_bf1[c][:].rearrange("p j t -> p (j t)"))
+
+            def en8_passes(g):
+                for place, nt in enumerate(groups[g][1]):
                     cols = slice(nt * P, (nt + 1) * P)
                     nc.tensor.matmul_mx(
                         out=y[g][:, place, :], lhsT=en8_w[:, cols].bitcast(FP8X4), lhsT_scale=en_s[EN8_ROW:, cols],
-                        rhs=h_w0[:, half].bitcast(FP8X4), rhs_scale=h_s[0][:, half], start=(place == 0), stop=False,
+                        rhs=h_w0[:].bitcast(FP8X4), rhs_scale=h_s[0][:, half], start=(place == 0), stop=False,
                     )
-            quantise(h_w1[:, half], h_s[1][:, half], h_bf1[:, half, :].rearrange("p j t -> p (j t)"))
+
+            if jh == 0:
+                for g in range(len(groups)):
+                    en8_passes(g)
             for g, (bank, nts) in enumerate(groups):
+                if jh == 1:
+                    en8_passes(g)
                 for c in (2 * jh, 2 * jh + 1):
                     js = slice(c * CHUNK, (c + 1) * CHUNK)
                     for place, nt in enumerate(nts):
@@ -204,9 +213,7 @@ def tile_list_kg_relu_mix_sig_kernel(
                             rhs=h_w1[:, js].bitcast(FP8X4), rhs_scale=h_s[1][:, js],
                             start=False, stop=(c % 2 == 1 and place == len(nts) - 1),
                         )
-                res = tile("res%d_%d" % (jh, nts[0]), [P, len(nts), JH], F32)
-                last = jh == 1 and g == len(groups) - 1
-                for first, count in ((0, 1), (1, 1)) if last else ((0, len(nts)),):
-                    part = slice(first, first + count)
-                    nc.scalar.activation(res[:, part], y[g][:, part], ACT.Sigmoid)
-                    nc.sync.dma_start(out_rows[:, nts[0] + first : nts[0] + first + count, half], res[:, part])
+                for place, nt in enumerate(nts):
+                    res = tile("res%d_%d" % (jh, nt), [P, JH], F32)
+                    nc.scalar.activation(res[:], y[g][:, place, :], ACT.Sigmoid)
+                    nc.sync.dma_start(out_rows[:, nt, half], res[:])

@@ -23,6 +23,8 @@ CHUNK = 128
 CHUNKS = J // CHUNK
 QUARTER = PASS // 2
 QM = QUARTER // PACK
+EM = QM // 2
+WB_PIECES = ((0, 384), (384, 384), (768, 256))
 NT = N // P
 JH = J // 2
 
@@ -58,8 +60,7 @@ def tile_list_kg_relu_mix_sig_kernel(
         en8_w = tile("en8_w", [P, N], I32)
         en4_w = tile("en4_w", [P, 2 * N], U8)
         en_s = tile("en_s", [P, N], U8)
-        wb_raw0 = tile("wb_raw0", [P, PACK, PASS], F32)
-        wb_raw1 = [tile("wb_raw1_%d" % q, [P, PACK, QUARTER], F32) for q in range(2)]
+        wb_raw = [tile("wb_raw%d" % n, [P, PACK, width], F32) for n, (first, width) in enumerate(WB_PIECES)]
         warm_in = tile("warm_in", [P, 1], F32)
         warm_out = tile("warm_out", [P, 1], F32)
 
@@ -91,10 +92,10 @@ def tile_list_kg_relu_mix_sig_kernel(
         for quad in range(4):
             load_wa_scales(quad, nc.sync)
         nc.sync.dma_start(idx2[:], offs2)
-        load_wb(wb_raw0, 0, PASS)
+        load_wb(wb_raw[0], *WB_PIECES[0])
         load_scales(tab2_s, TAB2_ROW, tab2_scales, nc.sync)
-        for q in range(2):
-            load_wb(wb_raw1[q], PASS + q * QUARTER, QUARTER)
+        for n in (1, 2):
+            load_wb(wb_raw[n], *WB_PIECES[n])
         nc.sync.dma_start(en4_w[:].bitcast(I32), en4_words[0].bitcast(I32))
         load_scales(en_s, EN4_ROW, en4_scales, nc.sync)
         load_words(en8_w, en8_words)
@@ -151,17 +152,19 @@ def tile_list_kg_relu_mix_sig_kernel(
         wa_pw.append(tile("wa_pw1", [P, PASS], I32, slot="wa_s"))
         deal_wa_words(1)
         nc.vector.tensor_copy(v2_w[:], tab2_w[:].bitcast(U32).indirect(idx2[:]))
-        raw0 = wb_raw0[:].rearrange("p i (m t) -> p i m t", t=PACK)
-        raw1 = [raw[:].rearrange("p i (m t) -> p i m t", t=PACK) for raw in wb_raw1]
-        round_wb(wb_bf[0][:, 0:2], raw0[:, :, :, 0:2], nc.vector.tensor_copy)
-        round_wb(wb_bf[0][:, 2:4], raw0[:, :, :, 2:4], nc.scalar.copy)
-        round_wb(wb_bf[1][:, :, 0:QM], raw1[0], nc.scalar.copy)
+        raw = [r[:].rearrange("p i (m t) -> p i m t", t=PACK) for r in wb_raw]
         nc.vector.tensor_copy(v2_s[:], tab2_s[:].indirect(idx2[:]))
-        wb_s = [tile("wb_s0", [P, PASS], U8, slot="tab2_s"), tile("wb_s1", [P, PASS], U8)]
+        wb_s = [tile("wb_s%d" % b, [P, PASS], U8) for b in range(HALVES)]
+        round_wb(wb_bf[0][:, :, 0 : P - EM], raw[0], nc.scalar.copy)
+        round_wb(wb_bf[1][:, :, 0:QM], raw[1][:, :, EM:], nc.scalar.copy)
+        for t in (0, 2):
+            round_wb(wb_bf[0][:, t : t + 2, P - EM : P], raw[1][:, :, 0:EM, t : t + 2], nc.vector.tensor_copy)
         quantise_wb(0)
         for t in (0, 2):
-            round_wb(wb_bf[1][:, t : t + 2, QM:P], raw1[1][:, :, :, t : t + 2], nc.vector.tensor_copy)
-        quantise_wb(1)
+            round_wb(wb_bf[1][:, t : t + 2, QM:P], raw[2][:, :, :, t : t + 2], nc.vector.tensor_copy)
+        for t in range(PACK):
+            cols = slice(t * P, (t + 1) * P)
+            quantise(wb_w[1][:, cols], wb_s[1][:, cols], wb_bf[1][:, t].rearrange("p m i -> p (m i)"))
         for b in range(HALVES):
             for c in range(CHUNKS):
                 js = slice(c * CHUNK, (c + 1) * CHUNK)
@@ -170,7 +173,7 @@ def tile_list_kg_relu_mix_sig_kernel(
                 js = slice(c * CHUNK, (c + 1) * CHUNK)
                 z_passes(b, c, wb_w[b][:], wb_s[b][:], v2_w[:, js], v2_s[TAB2_ROW:, js], first=False)
 
-        h_bf0 = [tile("h_bf0_%d" % jh, [P, JH, PACK], BF16, slot=slot) for jh, slot in enumerate(("wb_raw1_0", "wb_raw1_1"))]
+        h_bf0 = [tile("h_bf0_%d" % jh, [P, JH, PACK], BF16, slot=slot) for jh, slot in enumerate(("wb_raw1", "wb_raw2"))]
         h_bf1 = [tile("h_bf1_%d" % c, [P, CHUNK, PACK], BF16) for c in range(CHUNKS)]
         h_w1 = tile("h_w1", [P, J], U32)
         for c in range(CHUNKS):

@@ -29,7 +29,7 @@ NT = N // P
 JH = J // 2
 
 TAB_ROW, TAB2_ROW = 12, 8
-WA_ROW = (0, 4)
+WA_ROW = 4
 EN8_ROW, EN4_ROW = 4, 0
 Y_GROUPS = (
     (("bank0_0", (0,)), ("bank0_1", (1,)), ("bank0_2", (2, 3))),
@@ -56,7 +56,7 @@ def tile_list_kg_relu_mix_sig_kernel(
         tab2_w = tile("tab2_w", [P, T], I32)
         tab2_s = tile("tab2_s", [P, T], U8)
         wa_w = tile("wa_w", [P, R], I32)
-        wa_s = tile("wa_s", [P, PASS], U8)
+        wa_s = tile("wa_s", [P, R], U8)
         en8_w = tile("en8_w", [P, N], I32)
         en4_w = tile("en4_w", [P, 2 * N], U8)
         en_s = tile("en_s", [P, N], U8)
@@ -80,17 +80,12 @@ def tile_list_kg_relu_mix_sig_kernel(
             rows = wb.rearrange("(p i) r -> p i r", i=PACK)
             nc.sync.dma_start(dst[:], rows[:, :, first : first + width])
 
-        def load_wa_scales(quad, eng):
-            src = wa_scales[0, 4 * quad : 4 * quad + 4, :].bitcast(I32).rearrange("r (b n) -> b r n", b=HALVES)
-            eng.dma_start(wa_s[32 * quad : 32 * quad + 8, :].bitcast(I32), src)
-
         load_words(tab_w, tab_words)
         nc.sync.dma_start(idx[:], offs)
         load_scales(tab_s, TAB_ROW, tab_scales, nc.sync)
         load_words(wa_w, wa_words)
         load_words(tab2_w, tab2_words)
-        for quad in range(4):
-            load_wa_scales(quad, nc.sync)
+        load_scales(wa_s, WA_ROW, wa_scales, nc.sync)
         nc.sync.dma_start(idx2[:], offs2)
         load_wb(wb_raw[0], *WB_PIECES[0])
         load_scales(tab2_s, TAB2_ROW, tab2_scales, nc.sync)
@@ -105,17 +100,17 @@ def tile_list_kg_relu_mix_sig_kernel(
         v_s = tile("v_s", [P, J], U8)
         v2_w = tile("v2_w", [P, J], U32)
         v2_s = tile("v2_s", [P, J], U8)
-        wa_pw = [tile("wa_pw0", [P, PASS], I32)]
-        wa_ps = tile("wa_ps", [P, PASS], U8)
+        wa_pw = [tile("wa_pw%d" % b, [P, PASS], U32) for b in range(HALVES)]
+        wa_ps = [tile("wa_ps%d" % b, [P, PASS], U8) for b in range(HALVES)]
         wb_bf = [tile("wb_bf%d" % b, [P, PACK, P, PACK], BF16) for b in range(HALVES)]
         wb_w = [tile("wb_w%d" % b, [P, PASS], U32) for b in range(HALVES)]
         h_s = [tile("h_s%d" % b, [P, J], U8) for b in range(HALVES)]
         z = [[ps.tile([P, PACK, CHUNK], F32, name="z%d_%d" % (b, c), tag="bank%d_%d" % (b, c)) for c in range(CHUNKS)] for b in range(HALVES)]
 
         def deal_wa_words(b):
-            nc.vector.tensor_copy(
+            nc.scalar.copy(
                 wa_pw[b][:].rearrange("p (t g m) -> p g t m", t=PACK, m=4),
-                wa_w[:, b * PASS : (b + 1) * PASS].rearrange("p (g m t) -> p g t m", t=PACK, m=4),
+                wa_w[:, b * PASS : (b + 1) * PASS].bitcast(U32).rearrange("p (g m t) -> p g t m", t=PACK, m=4),
             )
 
         def round_wb(dst, raw, copy):
@@ -148,8 +143,11 @@ def tile_list_kg_relu_mix_sig_kernel(
         nc.vector.tensor_copy(v_w[:], tab_w[:].bitcast(U32).indirect(idx[:]))
         nc.vector.tensor_copy(v_s[:], tab_s[:].indirect(idx[:]))
         deal_wa_words(0)
-        nc.vector.tensor_copy(wa_ps[:].rearrange("p (t m) -> p t m", t=PACK), wa_s[:].rearrange("p (m t) -> p t m", t=PACK))
-        wa_pw.append(tile("wa_pw1", [P, PASS], I32, slot="wa_s"))
+        for b in range(HALVES):
+            nc.vector.tensor_copy(
+                wa_ps[b][:].rearrange("p (t m) -> p t m", t=PACK),
+                wa_s[:, b * PASS : (b + 1) * PASS].rearrange("p (m t) -> p t m", t=PACK),
+            )
         deal_wa_words(1)
         nc.vector.tensor_copy(v2_w[:], tab2_w[:].bitcast(U32).indirect(idx2[:]))
         raw = [r[:].rearrange("p i (m t) -> p i m t", t=PACK) for r in wb_raw]
@@ -168,7 +166,7 @@ def tile_list_kg_relu_mix_sig_kernel(
         for b in range(HALVES):
             for c in range(CHUNKS):
                 js = slice(c * CHUNK, (c + 1) * CHUNK)
-                z_passes(b, c, wa_pw[b][:], wa_ps[WA_ROW[b] :, :], v_w[:, js], v_s[TAB_ROW:, js], first=True)
+                z_passes(b, c, wa_pw[b][:], wa_ps[b][WA_ROW:, :], v_w[:, js], v_s[TAB_ROW:, js], first=True)
             for c in range(CHUNKS):
                 js = slice(c * CHUNK, (c + 1) * CHUNK)
                 z_passes(b, c, wb_w[b][:], wb_s[b][:], v2_w[:, js], v2_s[TAB2_ROW:, js], first=False)

@@ -18,23 +18,17 @@ ACT = mybir.ActivationFunctionType
 P = 128
 PACK = 4
 PASS = P * PACK
-HALVES = R // PASS
 CHUNK = 128
 CHUNKS = J // CHUNK
-QUARTER = PASS // 2
-QM = QUARTER // PACK
-EM = QM // 2
-WB_PIECES = ((0, 384), (384, 384), (768, 256))
+PIECE = PASS // 2
+PM = PIECE // PACK
 NT = N // P
 JH = J // 2
 
+FIRST, LAST = 1, 0
 TAB_ROW, TAB2_ROW = 12, 8
 WA_ROW = 4
 EN8_ROW, EN4_ROW = 4, 0
-Y_GROUPS = (
-    (("bank0_0", (0,)), ("bank0_1", (1,)), ("bank0_2", (2, 3))),
-    (("bank0_3", (0, 1)), ("bank1_0", (2, 3))),
-)
 
 
 def tile_list_kg_relu_mix_sig_kernel(
@@ -59,15 +53,16 @@ def tile_list_kg_relu_mix_sig_kernel(
         wa_s = tile("wa_s", [P, R], U8)
         en8_w = tile("en8_w", [P, N], I32)
         en4_w = tile("en4_w", [P, 2 * N], U8)
-        en_s = tile("en_s", [P, N], U8)
-        wb_raw = [tile("wb_raw%d" % n, [P, PACK, width], F32) for n, (first, width) in enumerate(WB_PIECES)]
+        en8_s = tile("en8_s", [P, N], U8)
+        en4_s = tile("en4_s", [P, N], U8)
+        wb_raw = {(b, n): tile("wb_raw%d_%d" % (b, n), [P, PACK, PIECE], F32) for b in (FIRST, LAST) for n in range(2)}
         warm_in = tile("warm_in", [P, 1], F32)
         warm_out = tile("warm_out", [P, 1], F32)
 
-        for plane in (tab_s, wa_s, tab2_s, en_s):
-            nc.vector.memset(plane[:].bitcast(I32), 0)
+        nc.vector.memset(tab_s[:].bitcast(I32), 0)
         nc.vector.memset(warm_in[:], 0.0)
-        nc.scalar.activation(warm_out[:], warm_in[:], ACT.Sigmoid)
+        for plane in (wa_s, tab2_s, en4_s, en8_s):
+            nc.vector.memset(plane[:].bitcast(I32), 0)
 
         def load_words(dst, src):
             nc.sync.dma_start(dst[:], src[0].rearrange("p n i -> p (n i)").bitcast(I32))
@@ -76,36 +71,39 @@ def tile_list_kg_relu_mix_sig_kernel(
             for r in range(4):
                 eng.dma_start(dst[row + r : P : 32, :].bitcast(I32), src[0, r:16:4, :].bitcast(I32))
 
-        def load_wb(dst, first, width):
+        def load_wb(b, n):
+            first = b * PASS + n * PIECE
             rows = wb.rearrange("(p i) r -> p i r", i=PACK)
-            nc.sync.dma_start(dst[:], rows[:, :, first : first + width])
+            nc.sync.dma_start(wb_raw[b, n][:], rows[:, :, first : first + PIECE])
 
-        load_words(tab_w, tab_words)
         nc.sync.dma_start(idx[:], offs)
-        load_scales(tab_s, TAB_ROW, tab_scales, nc.sync)
+        nc.sync.dma_start(idx2[:], offs2)
+        load_words(tab_w, tab_words)
         load_words(wa_w, wa_words)
         load_words(tab2_w, tab2_words)
-        load_scales(wa_s, WA_ROW, wa_scales, nc.sync)
-        nc.sync.dma_start(idx2[:], offs2)
-        load_wb(wb_raw[0], *WB_PIECES[0])
-        load_scales(tab2_s, TAB2_ROW, tab2_scales, nc.sync)
-        for n in (1, 2):
-            load_wb(wb_raw[n], *WB_PIECES[n])
+        for b in (FIRST, LAST):
+            for n in range(2):
+                load_wb(b, n)
+        load_scales(tab_s, TAB_ROW, tab_scales, nc.scalar)
+        nc.scalar.activation(warm_out[:], warm_in[:], ACT.Sigmoid)
+        load_scales(wa_s, WA_ROW, wa_scales, nc.scalar)
+        load_scales(tab2_s, TAB2_ROW, tab2_scales, nc.scalar)
+        load_scales(en4_s, EN4_ROW, en4_scales, nc.sync)
         nc.sync.dma_start(en4_w[:].bitcast(I32), en4_words[0].bitcast(I32))
-        load_scales(en_s, EN4_ROW, en4_scales, nc.sync)
         load_words(en8_w, en8_words)
-        load_scales(en_s, EN8_ROW, en8_scales, nc.sync)
+        load_scales(en8_s, EN8_ROW, en8_scales, nc.sync)
 
-        v_w = tile("v_w", [P, J], U32)
         v_s = tile("v_s", [P, J], U8)
-        v2_w = tile("v2_w", [P, J], U32)
-        v2_s = tile("v2_s", [P, J], U8)
-        wa_pw = [tile("wa_pw%d" % b, [P, PASS], U32) for b in range(HALVES)]
-        wa_ps = [tile("wa_ps%d" % b, [P, PASS], U8) for b in range(HALVES)]
-        wb_bf = [tile("wb_bf%d" % b, [P, PACK, P, PACK], BF16) for b in range(HALVES)]
-        wb_w = [tile("wb_w%d" % b, [P, PASS], U32) for b in range(HALVES)]
-        h_s = [tile("h_s%d" % b, [P, J], U8) for b in range(HALVES)]
-        z = [[ps.tile([P, PACK, CHUNK], F32, name="z%d_%d" % (b, c), tag="bank%d_%d" % (b, c)) for c in range(CHUNKS)] for b in range(HALVES)]
+        v_w = tile("v_w", [P, J], U32, slot="tab_s")
+        wa_pw = {b: tile("wa_pw%d" % b, [P, PASS], U32) for b in (FIRST, LAST)}
+        wa_ps = tile("wa_ps", [P, R], U8, slot="tab_w")
+        v2_w = tile("v2_w", [P, J], U32, slot="wa_s")
+        v2_s = tile("v2_s", [P, J], U8, slot="tab2_w")
+        wb_w = {b: tile("wb_w%d" % b, [P, PASS], U32) for b in (FIRST, LAST)}
+        wb_s = {b: tile("wb_s%d" % b, [P, PASS], U8) for b in (FIRST, LAST)}
+        h_s = {b: tile("h_s%d" % b, [P, J], U8) for b in (FIRST, LAST)}
+        h_w = {b: tile("h_w%d" % b, [P, J], U32) for b in (FIRST, LAST)}
+        z = {(b, c): ps.tile([P, PACK, CHUNK], F32, name="z%d_%d" % (b, c), tag="bank%d_%d" % (b, c)) for b in (FIRST, LAST) for c in range(CHUNKS)}
 
         def deal_wa_words(b):
             nc.scalar.copy(
@@ -119,102 +117,99 @@ def tile_list_kg_relu_mix_sig_kernel(
         def quantise(words, scales, values):
             nc.vector.quantize_mx(out=words.bitcast(FP8X4), scales=scales, in_=values)
 
-        def quantise_wb(b):
-            for t in (0, 2):
-                cols = slice(t * P, (t + 2) * P)
-                quantise(wb_w[b][:, cols], wb_s[b][:, cols], wb_bf[b][:, t : t + 2].rearrange("p t m i -> p (t m i)"))
+        def quantise_wb(b, tiles):
+            for t in range(0, PACK, tiles):
+                cols = slice(t * P, (t + tiles) * P)
+                quantise(wb_w[b][:, cols], wb_s[b][:, cols], wb_bf[b][:, t : t + tiles].rearrange("p t m i -> p (t m i)"))
 
         def z_passes(b, c, lhs_w, lhs_s, rhs_w, rhs_s, first):
             for t in range(PACK):
                 cols = slice(t * P, (t + 1) * P)
                 nc.tensor.matmul_mx(
-                    out=z[b][c][:, t, :], lhsT=lhs_w[:, cols].bitcast(FP8X4), lhsT_scale=lhs_s[:, cols],
+                    out=z[b, c][:, t, :], lhsT=lhs_w[:, cols].bitcast(FP8X4), lhsT_scale=lhs_s[:, cols],
                     rhs=rhs_w.bitcast(FP8X4), rhs_scale=rhs_s,
                     start=(first and t == 0), stop=(not first and t == PACK - 1),
                 )
 
+        def wa_passes(b):
+            for c in range(CHUNKS):
+                js = slice(c * CHUNK, (c + 1) * CHUNK)
+                z_passes(b, c, wa_pw[b][:], wa_ps[WA_ROW:, b * PASS : (b + 1) * PASS], v_w[:, js], v_s[TAB_ROW:, js], first=True)
+
+        def wb_passes(b):
+            for c in range(CHUNKS):
+                js = slice(c * CHUNK, (c + 1) * CHUNK)
+                z_passes(b, c, wb_w[b][:], wb_s[b][:], v2_w[:, js], v2_s[TAB2_ROW:, js], first=False)
+
         def relu(dst, b, c, on_scalar):
-            src = z[b][c][:].rearrange("p t j -> p j t")
+            src = z[b, c][:].rearrange("p t j -> p j t")
             if on_scalar:
                 nc.scalar.activation(dst, src, ACT.Relu)
             else:
                 nc.vector.tensor_scalar_max(dst, src, 0.0)
 
-        nc.vector.tensor_copy(v_w[:], tab_w[:].bitcast(U32).indirect(idx[:]))
         nc.vector.tensor_copy(v_s[:], tab_s[:].indirect(idx[:]))
-        deal_wa_words(0)
-        for b in range(HALVES):
+        nc.vector.tensor_copy(v_w[:], tab_w[:].bitcast(U32).indirect(idx[:]))
+        for b in (FIRST, LAST):
+            half = slice(b * PASS, (b + 1) * PASS)
+            deal_wa_words(b)
             nc.vector.tensor_copy(
-                wa_ps[b][:].rearrange("p (t m) -> p t m", t=PACK),
-                wa_s[:, b * PASS : (b + 1) * PASS].rearrange("p (m t) -> p t m", t=PACK),
+                wa_ps[:, half].rearrange("p (t m) -> p t m", t=PACK),
+                wa_s[:, half].rearrange("p (m t) -> p t m", t=PACK),
             )
-        deal_wa_words(1)
         nc.vector.tensor_copy(v2_w[:], tab2_w[:].bitcast(U32).indirect(idx2[:]))
-        raw = [r[:].rearrange("p i (m t) -> p i m t", t=PACK) for r in wb_raw]
         nc.vector.tensor_copy(v2_s[:], tab2_s[:].indirect(idx2[:]))
-        wb_s = [tile("wb_s%d" % b, [P, PASS], U8) for b in range(HALVES)]
-        round_wb(wb_bf[0][:, :, 0 : P - EM], raw[0], nc.scalar.copy)
-        round_wb(wb_bf[1][:, :, 0:QM], raw[1][:, :, EM:], nc.scalar.copy)
-        for t in (0, 2):
-            round_wb(wb_bf[0][:, t : t + 2, P - EM : P], raw[1][:, :, 0:EM, t : t + 2], nc.vector.tensor_copy)
-        quantise_wb(0)
-        for t in (0, 2):
-            round_wb(wb_bf[1][:, t : t + 2, QM:P], raw[2][:, :, :, t : t + 2], nc.vector.tensor_copy)
-        for t in range(PACK):
-            cols = slice(t * P, (t + 1) * P)
-            quantise(wb_w[1][:, cols], wb_s[1][:, cols], wb_bf[1][:, t].rearrange("p m i -> p (m i)"))
-        for b in range(HALVES):
-            for c in range(CHUNKS):
-                js = slice(c * CHUNK, (c + 1) * CHUNK)
-                z_passes(b, c, wa_pw[b][:], wa_ps[b][WA_ROW:, :], v_w[:, js], v_s[TAB_ROW:, js], first=True)
-            for c in range(CHUNKS):
-                js = slice(c * CHUNK, (c + 1) * CHUNK)
-                z_passes(b, c, wb_w[b][:], wb_s[b][:], v2_w[:, js], v2_s[TAB2_ROW:, js], first=False)
+        raw = {key: r[:].rearrange("p i (m t) -> p i m t", t=PACK) for key, r in wb_raw.items()}
+        wb_bf = {b: tile("wb_bf%d" % b, [P, PACK, P, PACK], BF16) for b in (FIRST, LAST)}
 
-        h_bf0 = [tile("h_bf0_%d" % jh, [P, JH, PACK], BF16, slot=slot) for jh, slot in enumerate(("wb_raw1", "wb_raw2"))]
-        h_bf1 = [tile("h_bf1_%d" % c, [P, CHUNK, PACK], BF16) for c in range(CHUNKS)]
-        h_w1 = tile("h_w1", [P, J], U32)
+        round_wb(wb_bf[FIRST][:, :, 0:PM], raw[FIRST, 0], nc.scalar.copy)
+        round_wb(wb_bf[FIRST][:, 2:4, PM:P], raw[FIRST, 1][:, :, :, 2:4], nc.scalar.copy)
+        round_wb(wb_bf[FIRST][:, 0:2, PM:P], raw[FIRST, 1][:, :, :, 0:2], nc.vector.tensor_copy)
+        quantise_wb(FIRST, 2)
+        round_wb(wb_bf[LAST][:, :, 0:PM], raw[LAST, 0], nc.vector.tensor_copy)
+        for t in (0, 2):
+            round_wb(wb_bf[LAST][:, t : t + 2, PM:P], raw[LAST, 1][:, :, :, t : t + 2], nc.vector.tensor_copy)
+        quantise_wb(LAST, 1)
+        wa_passes(FIRST)
+        wa_passes(LAST)
+        wb_passes(FIRST)
+        wb_passes(LAST)
+
+        h_first = [tile("h_first%d" % jh, [P, JH, PACK], BF16) for jh in range(2)]
+        h_last = [tile("h_last%d" % c, [P, CHUNK, PACK], BF16) for c in range(CHUNKS)]
         for c in range(CHUNKS):
-            relu(h_bf0[c // 2][:, c % 2 * CHUNK : (c % 2 + 1) * CHUNK, :], 0, c, on_scalar=(c != 3))
+            relu(h_first[c // 2][:, c % 2 * CHUNK : (c % 2 + 1) * CHUNK, :], FIRST, c, on_scalar=True)
+        for jh in range(2):
+            half = slice(jh * JH, (jh + 1) * JH)
+            quantise(h_w[FIRST][:, half], h_s[FIRST][:, half], h_first[jh][:].rearrange("p j t -> p (j t)"))
 
         out_rows = out.rearrange("(nt p) j -> p nt j", p=P)
         for jh in range(2):
             half = slice(jh * JH, (jh + 1) * JH)
-            for c in (2 * jh, 2 * jh + 1):
-                relu(h_bf1[c][:], 1, c, on_scalar=(c != 1))
-            h_w0 = tile("h_w0_%d" % jh, [P, JH], U32, slot=("wb_bf1", "h_bf1_1")[jh])
-            quantise(h_w0[:], h_s[0][:, half], h_bf0[jh][:].rearrange("p j t -> p (j t)"))
-            groups = Y_GROUPS[jh]
-            y = [ps.tile([P, len(nts), JH], F32, name="y%d_%d" % (jh, nts[0]), tag=bank) for bank, nts in groups]
-            for c in (2 * jh, 2 * jh + 1):
+            chunks = (2 * jh, 2 * jh + 1)
+            for c in chunks:
+                relu(h_last[c][:], LAST, c, on_scalar=(c % 2 == 0))
+            for c in chunks:
                 js = slice(c * CHUNK, (c + 1) * CHUNK)
-                quantise(h_w1[:, js], h_s[1][:, js], h_bf1[c][:].rearrange("p j t -> p (j t)"))
-
-            def en8_passes(g):
-                for place, nt in enumerate(groups[g][1]):
+                quantise(h_w[LAST][:, js], h_s[LAST][:, js], h_last[c][:].rearrange("p j t -> p (j t)"))
+            y = [ps.tile([P, 2, JH], F32, name="y%d_%d" % (jh, g), tag="bank%d_%d" % (FIRST, 2 * jh + g)) for g in range(2)]
+            for nt in range(NT):
+                nc.tensor.matmul_mx(
+                    out=y[nt // 2][:, nt % 2, :], lhsT=en4_w[:, 2 * nt * P : 2 * (nt + 1) * P].bitcast(FP4X4),
+                    lhsT_scale=en4_s[EN4_ROW:, nt * P : (nt + 1) * P],
+                    rhs=h_w[FIRST][:, half].bitcast(FP8X4), rhs_scale=h_s[FIRST][:, half], start=(nt % 2 == 0), stop=False,
+                )
+            for c in chunks:
+                js = slice(c * CHUNK, (c + 1) * CHUNK)
+                for nt in range(NT):
                     cols = slice(nt * P, (nt + 1) * P)
                     nc.tensor.matmul_mx(
-                        out=y[g][:, place, :], lhsT=en8_w[:, cols].bitcast(FP8X4), lhsT_scale=en_s[EN8_ROW:, cols],
-                        rhs=h_w0[:].bitcast(FP8X4), rhs_scale=h_s[0][:, half], start=(place == 0), stop=False,
+                        out=y[nt // 2][:, nt % 2, c % 2 * CHUNK : (c % 2 + 1) * CHUNK],
+                        lhsT=en8_w[:, cols].bitcast(FP8X4), lhsT_scale=en8_s[EN8_ROW:, cols],
+                        rhs=h_w[LAST][:, js].bitcast(FP8X4), rhs_scale=h_s[LAST][:, js],
+                        start=False, stop=(c % 2 == 1 and nt % 2 == 1),
                     )
-
-            if jh == 0:
-                for g in range(len(groups)):
-                    en8_passes(g)
-            for g, (bank, nts) in enumerate(groups):
-                if jh == 1:
-                    en8_passes(g)
-                for c in (2 * jh, 2 * jh + 1):
-                    js = slice(c * CHUNK, (c + 1) * CHUNK)
-                    for place, nt in enumerate(nts):
-                        nc.tensor.matmul_mx(
-                            out=y[g][:, place, c % 2 * CHUNK : (c % 2 + 1) * CHUNK],
-                            lhsT=en4_w[:, 2 * nt * P : 2 * (nt + 1) * P].bitcast(FP4X4),
-                            lhsT_scale=en_s[EN4_ROW:, nt * P : (nt + 1) * P],
-                            rhs=h_w1[:, js].bitcast(FP8X4), rhs_scale=h_s[1][:, js],
-                            start=False, stop=(c % 2 == 1 and place == len(nts) - 1),
-                        )
-                for place, nt in enumerate(nts):
-                    res = tile("res%d_%d" % (jh, nt), [P, JH], F32)
-                    nc.scalar.activation(res[:], y[g][:, place, :], ACT.Sigmoid)
-                    nc.sync.dma_start(out_rows[:, nt, half], res[:])
+            for nt in range(NT):
+                res = tile("res%d_%d" % (jh, nt), [P, JH], F32)
+                nc.scalar.activation(res[:], y[nt // 2][:, nt % 2, :], ACT.Sigmoid)
+                nc.sync.dma_start(out_rows[:, nt, half], res[:])

@@ -59,10 +59,10 @@ def tile_list_kg_relu_mix_sig_kernel(
         warm_in = tile("warm_in", [P, 1], F32)
         warm_out = tile("warm_out", [P, 1], F32)
 
-        nc.vector.memset(tab_s[:].bitcast(I32), 0)
-        nc.vector.memset(warm_in[:], 0.0)
-        for plane in (wa_s, tab2_s, en4_s, en8_s):
+        for plane in (tab2_s, wa_s, tab_s, en4_s, en8_s):
             nc.vector.memset(plane[:].bitcast(I32), 0)
+        nc.vector.memset(warm_in[:], 0.0)
+        nc.scalar.activation(warm_out[:], warm_in[:], ACT.Sigmoid)
 
         def load_words(dst, src):
             nc.sync.dma_start(dst[:], src[0].rearrange("p n i -> p (n i)").bitcast(I32))
@@ -76,33 +76,32 @@ def tile_list_kg_relu_mix_sig_kernel(
             rows = wb.rearrange("(p i) r -> p i r", i=PACK)
             nc.sync.dma_start(wb_raw[b, n][:], rows[:, :, first : first + PIECE])
 
-        nc.sync.dma_start(idx[:], offs)
+        load_words(tab2_w, tab2_words)
         nc.sync.dma_start(idx2[:], offs2)
+        load_scales(tab2_s, TAB2_ROW, tab2_scales, nc.sync)
+        load_wb(FIRST, 0)
+        load_wb(FIRST, 1)
+        nc.sync.dma_start(idx[:], offs)
+        load_scales(wa_s, WA_ROW, wa_scales, nc.sync)
         load_words(tab_w, tab_words)
         load_words(wa_w, wa_words)
-        load_words(tab2_w, tab2_words)
-        for b in (FIRST, LAST):
-            for n in range(2):
-                load_wb(b, n)
-        load_scales(tab_s, TAB_ROW, tab_scales, nc.scalar)
-        nc.scalar.activation(warm_out[:], warm_in[:], ACT.Sigmoid)
-        load_scales(wa_s, WA_ROW, wa_scales, nc.scalar)
-        load_scales(tab2_s, TAB2_ROW, tab2_scales, nc.scalar)
-        load_scales(en4_s, EN4_ROW, en4_scales, nc.sync)
-        nc.sync.dma_start(en4_w[:].bitcast(I32), en4_words[0].bitcast(I32))
-        load_words(en8_w, en8_words)
+        load_scales(tab_s, TAB_ROW, tab_scales, nc.sync)
+        load_wb(LAST, 0)
+        load_wb(LAST, 1)
         load_scales(en8_s, EN8_ROW, en8_scales, nc.sync)
+        load_words(en8_w, en8_words)
+        nc.sync.dma_start(en4_w[:].bitcast(I32), en4_words[0].bitcast(I32))
+        load_scales(en4_s, EN4_ROW, en4_scales, nc.sync)
 
         v_s = tile("v_s", [P, J], U8)
-        v_w = tile("v_w", [P, J], U32, slot="tab_s")
+        v_w = tile("v_w", [P, J], U32)
         wa_pw = {b: tile("wa_pw%d" % b, [P, PASS], U32) for b in (FIRST, LAST)}
-        wa_ps = tile("wa_ps", [P, R], U8, slot="tab_w")
-        v2_w = tile("v2_w", [P, J], U32, slot="wa_s")
-        v2_s = tile("v2_s", [P, J], U8, slot="tab2_w")
+        v2_w = tile("v2_w", [P, J], U32)
+        v2_s = tile("v2_s", [P, J], U8)
         wb_w = {b: tile("wb_w%d" % b, [P, PASS], U32) for b in (FIRST, LAST)}
         wb_s = {b: tile("wb_s%d" % b, [P, PASS], U8) for b in (FIRST, LAST)}
         h_s = {b: tile("h_s%d" % b, [P, J], U8) for b in (FIRST, LAST)}
-        h_w = {b: tile("h_w%d" % b, [P, J], U32) for b in (FIRST, LAST)}
+        h_w = {LAST: tile("h_w%d" % LAST, [P, J], U32)}
         z = {(b, c): ps.tile([P, PACK, CHUNK], F32, name="z%d_%d" % (b, c), tag="bank%d_%d" % (b, c)) for b in (FIRST, LAST) for c in range(CHUNKS)}
 
         def deal_wa_words(b):
@@ -123,23 +122,24 @@ def tile_list_kg_relu_mix_sig_kernel(
                 quantise(wb_w[b][:, cols], wb_s[b][:, cols], wb_bf[b][:, t : t + tiles].rearrange("p t m i -> p (t m i)"))
 
         def z_passes(b, c, lhs_w, lhs_s, rhs_w, rhs_s, first):
-            for t in range(PACK):
+            order = range(PACK) if b == FIRST or c < 2 else range(PACK - 1, -1, -1)
+            for t in order:
                 cols = slice(t * P, (t + 1) * P)
                 nc.tensor.matmul_mx(
                     out=z[b, c][:, t, :], lhsT=lhs_w[:, cols].bitcast(FP8X4), lhsT_scale=lhs_s[:, cols],
                     rhs=rhs_w.bitcast(FP8X4), rhs_scale=rhs_s,
-                    start=(first and t == 0), stop=(not first and t == PACK - 1),
+                    start=(first and t == order[0]), stop=(not first and t == order[-1]),
                 )
 
-        def wa_passes(b):
-            for c in range(CHUNKS):
+        def wa_passes(b, chunks):
+            for c in chunks:
                 js = slice(c * CHUNK, (c + 1) * CHUNK)
-                z_passes(b, c, wa_pw[b][:], wa_ps[WA_ROW:, b * PASS : (b + 1) * PASS], v_w[:, js], v_s[TAB_ROW:, js], first=True)
+                z_passes(b, c, wa_pw[b][:], wa_ps[WA_ROW:, b * PASS : (b + 1) * PASS], v_w[:, js], v_s[TAB_ROW:, js], first=(b == LAST and c < CHUNKS - 1))
 
-        def wb_passes(b):
-            for c in range(CHUNKS):
+        def wb_passes(b, chunks):
+            for c in chunks:
                 js = slice(c * CHUNK, (c + 1) * CHUNK)
-                z_passes(b, c, wb_w[b][:], wb_s[b][:], v2_w[:, js], v2_s[TAB2_ROW:, js], first=False)
+                z_passes(b, c, wb_w[b][:], wb_s[b][:], v2_w[:, js], v2_s[TAB2_ROW:, js], first=(b == FIRST or c == CHUNKS - 1))
 
         def relu(dst, b, c, on_scalar):
             src = z[b, c][:].rearrange("p t j -> p j t")
@@ -148,37 +148,42 @@ def tile_list_kg_relu_mix_sig_kernel(
             else:
                 nc.vector.tensor_scalar_max(dst, src, 0.0)
 
-        nc.vector.tensor_copy(v_s[:], tab_s[:].indirect(idx[:]))
-        nc.vector.tensor_copy(v_w[:], tab_w[:].bitcast(U32).indirect(idx[:]))
-        for b in (FIRST, LAST):
-            half = slice(b * PASS, (b + 1) * PASS)
-            deal_wa_words(b)
-            nc.vector.tensor_copy(
-                wa_ps[:, half].rearrange("p (t m) -> p t m", t=PACK),
-                wa_s[:, half].rearrange("p (m t) -> p t m", t=PACK),
-            )
-        nc.vector.tensor_copy(v2_w[:], tab2_w[:].bitcast(U32).indirect(idx2[:]))
-        nc.vector.tensor_copy(v2_s[:], tab2_s[:].indirect(idx2[:]))
         raw = {key: r[:].rearrange("p i (m t) -> p i m t", t=PACK) for key, r in wb_raw.items()}
         wb_bf = {b: tile("wb_bf%d" % b, [P, PACK, P, PACK], BF16) for b in (FIRST, LAST)}
-
+        nc.vector.tensor_copy(v2_w[:], tab2_w[:].bitcast(U32).indirect(idx2[:]))
+        nc.vector.tensor_copy(v2_s[:], tab2_s[:].indirect(idx2[:]))
         round_wb(wb_bf[FIRST][:, :, 0:PM], raw[FIRST, 0], nc.scalar.copy)
         round_wb(wb_bf[FIRST][:, 2:4, PM:P], raw[FIRST, 1][:, :, :, 2:4], nc.scalar.copy)
         round_wb(wb_bf[FIRST][:, 0:2, PM:P], raw[FIRST, 1][:, :, :, 0:2], nc.vector.tensor_copy)
-        quantise_wb(FIRST, 2)
+        quantise_wb(FIRST, 1)
+        wb_passes(FIRST, range(CHUNKS))
+        wa_ps = tile("wa_ps", [P, R], U8, slot="wb_bf%d" % FIRST)
+        nc.vector.tensor_copy(v_w[:], tab_w[:].bitcast(U32).indirect(idx[:]))
+        for first, last in ((0, CHUNK), (CHUNK, JH), (JH, J)):
+            nc.vector.tensor_copy(v_s[:, first:last], tab_s[:].indirect(idx[:, first // 16 : last // 16]))
+        for b in (FIRST, LAST):
+            half = slice(b * PASS, (b + 1) * PASS)
+            deal_wa_words(b)
+            nc.gpsimd.tensor_copy(
+                wa_ps[:, half].rearrange("p (t m) -> p t m", t=PACK),
+                wa_s[:, half].rearrange("p (m t) -> p t m", t=PACK),
+            )
+        wa_passes(FIRST, (0, 1))
+        wa_passes(LAST, (0, 1))
+        wa_passes(FIRST, (2, 3))
+        wa_passes(LAST, (2,))
         round_wb(wb_bf[LAST][:, :, 0:PM], raw[LAST, 0], nc.vector.tensor_copy)
         for t in (0, 2):
             round_wb(wb_bf[LAST][:, t : t + 2, PM:P], raw[LAST, 1][:, :, :, t : t + 2], nc.vector.tensor_copy)
         quantise_wb(LAST, 1)
-        wa_passes(FIRST)
-        wa_passes(LAST)
-        wb_passes(FIRST)
-        wb_passes(LAST)
+        wb_passes(LAST, range(CHUNKS))
+        wa_passes(LAST, (3,))
 
         h_first = [tile("h_first%d" % jh, [P, JH, PACK], BF16) for jh in range(2)]
-        h_last = [tile("h_last%d" % c, [P, CHUNK, PACK], BF16) for c in range(CHUNKS)]
+        h_last = {}
         for c in range(CHUNKS):
             relu(h_first[c // 2][:, c % 2 * CHUNK : (c % 2 + 1) * CHUNK, :], FIRST, c, on_scalar=True)
+        h_w[FIRST] = tile("h_w%d" % FIRST, [P, J], U32, slot="wb_raw%d_1" % LAST)
         for jh in range(2):
             half = slice(jh * JH, (jh + 1) * JH)
             quantise(h_w[FIRST][:, half], h_s[FIRST][:, half], h_first[jh][:].rearrange("p j t -> p (j t)"))
@@ -188,28 +193,29 @@ def tile_list_kg_relu_mix_sig_kernel(
             half = slice(jh * JH, (jh + 1) * JH)
             chunks = (2 * jh, 2 * jh + 1)
             for c in chunks:
+                h_last[c] = tile("h_last%d" % c, [P, CHUNK, PACK], BF16, slot="h_last%d" % (0 if c == 3 else c))
                 relu(h_last[c][:], LAST, c, on_scalar=(c % 2 == 0))
             for c in chunks:
                 js = slice(c * CHUNK, (c + 1) * CHUNK)
                 quantise(h_w[LAST][:, js], h_s[LAST][:, js], h_last[c][:].rearrange("p j t -> p (j t)"))
-            y = [ps.tile([P, 2, JH], F32, name="y%d_%d" % (jh, g), tag="bank%d_%d" % (FIRST, 2 * jh + g)) for g in range(2)]
+            share = jh + 1
+            y = [
+                ps.tile([P, share, JH], F32, name="y%d_%d" % (jh, g), tag="bank%d_%d" % ((FIRST, LAST)[jh], g))
+                for g in range(NT // share)
+            ]
             for nt in range(NT):
                 nc.tensor.matmul_mx(
-                    out=y[nt // 2][:, nt % 2, :], lhsT=en4_w[:, 2 * nt * P : 2 * (nt + 1) * P].bitcast(FP4X4),
+                    out=y[nt // share][:, nt % share, :], lhsT=en4_w[:, 2 * nt * P : 2 * (nt + 1) * P].bitcast(FP4X4),
                     lhsT_scale=en4_s[EN4_ROW:, nt * P : (nt + 1) * P],
-                    rhs=h_w[FIRST][:, half].bitcast(FP8X4), rhs_scale=h_s[FIRST][:, half], start=(nt % 2 == 0), stop=False,
+                    rhs=h_w[FIRST][:, half].bitcast(FP8X4), rhs_scale=h_s[FIRST][:, half], start=(nt % share == 0), stop=False,
                 )
-            for c in chunks:
-                js = slice(c * CHUNK, (c + 1) * CHUNK)
-                for nt in range(NT):
-                    cols = slice(nt * P, (nt + 1) * P)
-                    nc.tensor.matmul_mx(
-                        out=y[nt // 2][:, nt % 2, c % 2 * CHUNK : (c % 2 + 1) * CHUNK],
-                        lhsT=en8_w[:, cols].bitcast(FP8X4), lhsT_scale=en8_s[EN8_ROW:, cols],
-                        rhs=h_w[LAST][:, js].bitcast(FP8X4), rhs_scale=h_s[LAST][:, js],
-                        start=False, stop=(c % 2 == 1 and nt % 2 == 1),
-                    )
+            for nt in range(NT):
+                cols = slice(nt * P, (nt + 1) * P)
+                nc.tensor.matmul_mx(
+                    out=y[nt // share][:, nt % share, :], lhsT=en8_w[:, cols].bitcast(FP8X4), lhsT_scale=en8_s[EN8_ROW:, cols],
+                    rhs=h_w[LAST][:, half].bitcast(FP8X4), rhs_scale=h_s[LAST][:, half], start=False, stop=(nt % share == share - 1),
+                )
             for nt in range(NT):
                 res = tile("res%d_%d" % (jh, nt), [P, JH], F32)
-                nc.scalar.activation(res[:], y[nt // 2][:, nt % 2, :], ACT.Sigmoid)
+                nc.scalar.activation(res[:], y[nt // share][:, nt % share, :], ACT.Sigmoid)
                 nc.sync.dma_start(out_rows[:, nt, half], res[:])

@@ -29,6 +29,7 @@ FIRST, LAST = 1, 0
 TAB_ROW, TAB2_ROW = 12, 8
 WA_ROW = 4
 EN8_ROW, EN4_ROW = 4, 0
+Y_GROUPS = (((0,), (1,), (2,), (3,)), ((0,), (1,), (2, 3)))
 
 
 def tile_list_kg_relu_mix_sig_kernel(
@@ -183,39 +184,50 @@ def tile_list_kg_relu_mix_sig_kernel(
         h_last = {}
         for c in range(CHUNKS):
             relu(h_first[c // 2][:, c % 2 * CHUNK : (c % 2 + 1) * CHUNK, :], FIRST, c, on_scalar=True)
-        h_w[FIRST] = tile("h_w%d" % FIRST, [P, J], U32, slot="wb_raw%d_1" % LAST)
-        for jh in range(2):
-            half = slice(jh * JH, (jh + 1) * JH)
-            quantise(h_w[FIRST][:, half], h_s[FIRST][:, half], h_first[jh][:].rearrange("p j t -> p (j t)"))
 
         out_rows = out.rearrange("(nt p) j -> p nt j", p=P)
         for jh in range(2):
             half = slice(jh * JH, (jh + 1) * JH)
             chunks = (2 * jh, 2 * jh + 1)
+            first_w = tile("first_w%d" % jh, [P, JH], U32, slot=("wb_raw%d_1" % LAST, "h_last0")[jh])
+            quantise(first_w[:], h_s[FIRST][:, half], h_first[jh][:].rearrange("p j t -> p (j t)"))
             for c in chunks:
-                h_last[c] = tile("h_last%d" % c, [P, CHUNK, PACK], BF16, slot="h_last%d" % (0 if c == 3 else c))
+                h_last[c] = tile("h_last%d" % c, [P, CHUNK, PACK], BF16, slot="h_last%d" % (1 if c == 3 else c))
                 relu(h_last[c][:], LAST, c, on_scalar=(c % 2 == 0))
             for c in chunks:
                 js = slice(c * CHUNK, (c + 1) * CHUNK)
                 quantise(h_w[LAST][:, js], h_s[LAST][:, js], h_last[c][:].rearrange("p j t -> p (j t)"))
-            share = jh + 1
-            y = [
-                ps.tile([P, share, JH], F32, name="y%d_%d" % (jh, g), tag="bank%d_%d" % ((FIRST, LAST)[jh], g))
-                for g in range(NT // share)
-            ]
-            for nt in range(NT):
+            groups = Y_GROUPS[jh]
+            y, opens, closes = {}, set(), set()
+            for g, nts in enumerate(groups):
+                bank = ps.tile([P, len(nts), JH], F32, name="y%d_%d" % (jh, g), tag="bank%d_%d" % ((FIRST, LAST)[jh], g))
+                opens.add(nts[0])
+                closes.add(nts[-1])
+                for place, nt in enumerate(nts):
+                    y[nt] = bank[:, place, :]
+
+            def en4_pass(nt):
                 nc.tensor.matmul_mx(
-                    out=y[nt // share][:, nt % share, :], lhsT=en4_w[:, 2 * nt * P : 2 * (nt + 1) * P].bitcast(FP4X4),
+                    out=y[nt], lhsT=en4_w[:, 2 * nt * P : 2 * (nt + 1) * P].bitcast(FP4X4),
                     lhsT_scale=en4_s[EN4_ROW:, nt * P : (nt + 1) * P],
-                    rhs=h_w[FIRST][:, half].bitcast(FP8X4), rhs_scale=h_s[FIRST][:, half], start=(nt % share == 0), stop=False,
+                    rhs=first_w[:].bitcast(FP8X4), rhs_scale=h_s[FIRST][:, half], start=(nt in opens), stop=False,
                 )
-            for nt in range(NT):
+
+            def en8_pass(nt):
                 cols = slice(nt * P, (nt + 1) * P)
                 nc.tensor.matmul_mx(
-                    out=y[nt // share][:, nt % share, :], lhsT=en8_w[:, cols].bitcast(FP8X4), lhsT_scale=en8_s[EN8_ROW:, cols],
-                    rhs=h_w[LAST][:, half].bitcast(FP8X4), rhs_scale=h_s[LAST][:, half], start=False, stop=(nt % share == share - 1),
+                    out=y[nt], lhsT=en8_w[:, cols].bitcast(FP8X4), lhsT_scale=en8_s[EN8_ROW:, cols],
+                    rhs=h_w[LAST][:, half].bitcast(FP8X4), rhs_scale=h_s[LAST][:, half], start=False, stop=(nt in closes),
                 )
+
+            ahead = (2, 3)[jh]
+            for nt in range(ahead):
+                en4_pass(nt)
+            for nt in range(NT):
+                if nt >= ahead:
+                    en4_pass(nt)
+                en8_pass(nt)
             for nt in range(NT):
                 res = tile("res%d_%d" % (jh, nt), [P, JH], F32)
-                nc.scalar.activation(res[:], y[nt // share][:, nt % share, :], ACT.Sigmoid)
+                nc.scalar.activation(res[:], y[nt], ACT.Sigmoid)
                 nc.sync.dma_start(out_rows[:, nt, half], res[:])

@@ -29,7 +29,6 @@ FIRST, LAST = 1, 0
 TAB_ROW, TAB2_ROW = 12, 8
 WA_ROW = 4
 EN8_ROW, EN4_ROW = 4, 0
-Y_GROUPS = (((0,), (1,), (2,), (3,)), ((0,), (1,), (2, 3)))
 
 
 def tile_list_kg_relu_mix_sig_kernel(
@@ -186,48 +185,64 @@ def tile_list_kg_relu_mix_sig_kernel(
             relu(h_first[c // 2][:, c % 2 * CHUNK : (c % 2 + 1) * CHUNK, :], FIRST, c, on_scalar=True)
 
         out_rows = out.rearrange("(nt p) j -> p nt j", p=P)
-        for jh in range(2):
-            half = slice(jh * JH, (jh + 1) * JH)
-            chunks = (2 * jh, 2 * jh + 1)
-            first_w = tile("first_w%d" % jh, [P, JH], U32, slot=("wb_raw%d_1" % LAST, "h_last0")[jh])
-            quantise(first_w[:], h_s[FIRST][:, half], h_first[jh][:].rearrange("p j t -> p (j t)"))
+        early_w = tile("early_w", [P, JH + CHUNK], U32, slot="wb_raw%d_1" % LAST)
+        quantise(early_w[:, 0:JH], h_s[FIRST][:, 0:JH], h_first[0][:].rearrange("p j t -> p (j t)"))
+        quantise(early_w[:, JH:], h_s[FIRST][:, JH : JH + CHUNK], h_first[1][:, 0:CHUNK].rearrange("p j t -> p (j t)"))
+
+        def last_half(chunks):
             for c in chunks:
                 h_last[c] = tile("h_last%d" % c, [P, CHUNK, PACK], BF16, slot="h_last%d" % (1 if c == 3 else c))
                 relu(h_last[c][:], LAST, c, on_scalar=(c % 2 == 0))
             for c in chunks:
                 js = slice(c * CHUNK, (c + 1) * CHUNK)
                 quantise(h_w[LAST][:, js], h_s[LAST][:, js], h_last[c][:].rearrange("p j t -> p (j t)"))
-            groups = Y_GROUPS[jh]
-            y, opens, closes = {}, set(), set()
-            for g, nts in enumerate(groups):
-                bank = ps.tile([P, len(nts), JH], F32, name="y%d_%d" % (jh, g), tag="bank%d_%d" % ((FIRST, LAST)[jh], g))
-                opens.add(nts[0])
-                closes.add(nts[-1])
-                for place, nt in enumerate(nts):
-                    y[nt] = bank[:, place, :]
 
-            def en4_pass(nt):
-                nc.tensor.matmul_mx(
-                    out=y[nt], lhsT=en4_w[:, 2 * nt * P : 2 * (nt + 1) * P].bitcast(FP4X4),
-                    lhsT_scale=en4_s[EN4_ROW:, nt * P : (nt + 1) * P],
-                    rhs=first_w[:].bitcast(FP8X4), rhs_scale=h_s[FIRST][:, half], start=(nt in opens), stop=False,
-                )
+        def en4_pass(dst, nt, words, js, start):
+            nc.tensor.matmul_mx(
+                out=dst, lhsT=en4_w[:, 2 * nt * P : 2 * (nt + 1) * P].bitcast(FP4X4),
+                lhsT_scale=en4_s[EN4_ROW:, nt * P : (nt + 1) * P],
+                rhs=words.bitcast(FP8X4), rhs_scale=h_s[FIRST][:, js], start=start, stop=False,
+            )
 
-            def en8_pass(nt):
-                cols = slice(nt * P, (nt + 1) * P)
-                nc.tensor.matmul_mx(
-                    out=y[nt], lhsT=en8_w[:, cols].bitcast(FP8X4), lhsT_scale=en8_s[EN8_ROW:, cols],
-                    rhs=h_w[LAST][:, half].bitcast(FP8X4), rhs_scale=h_s[LAST][:, half], start=False, stop=(nt in closes),
-                )
+        def en8_pass(dst, nt, js, stop):
+            cols = slice(nt * P, (nt + 1) * P)
+            nc.tensor.matmul_mx(
+                out=dst, lhsT=en8_w[:, cols].bitcast(FP8X4), lhsT_scale=en8_s[EN8_ROW:, cols],
+                rhs=h_w[LAST][:, js].bitcast(FP8X4), rhs_scale=h_s[LAST][:, js], start=False, stop=stop,
+            )
 
-            ahead = (2, 3)[jh]
-            for nt in range(ahead):
-                en4_pass(nt)
-            for nt in range(NT):
-                if nt >= ahead:
-                    en4_pass(nt)
-                en8_pass(nt)
-            for nt in range(NT):
-                res = tile("res%d_%d" % (jh, nt), [P, JH], F32)
-                nc.scalar.activation(res[:], y[nt], ACT.Sigmoid)
-                nc.sync.dma_start(out_rows[:, nt, half], res[:])
+        def finish(src, nt, half):
+            res = tile("res%d_%d" % (half.start, nt), [P, JH], F32)
+            nc.scalar.activation(res[:], src, ACT.Sigmoid)
+            nc.sync.dma_start(out_rows[:, nt, half], res[:])
+
+        chunk = [slice(c * CHUNK, (c + 1) * CHUNK) for c in range(CHUNKS)]
+        half = slice(0, JH)
+        last_half((0, 1))
+        y = [ps.tile([P, JH], F32, name="y0_%d" % nt, tag="bank%d_%d" % (FIRST, nt)) for nt in range(NT)]
+        for nt in range(2):
+            en4_pass(y[nt][:], nt, early_w[:, half], half, start=True)
+        for nt in range(NT):
+            if nt >= 2:
+                en4_pass(y[nt][:], nt, early_w[:, half], half, start=True)
+            if nt == 0:
+                en8_pass(y[nt][:, chunk[0]], nt, chunk[0], stop=False)
+                en8_pass(y[nt][:, chunk[1]], nt, chunk[1], stop=True)
+            else:
+                en8_pass(y[nt][:], nt, half, stop=True)
+            finish(y[nt][:], nt, half)
+
+        half = slice(JH, J)
+        late_w = tile("late_w", [P, CHUNK], U32, slot="h_last0")
+        quantise(late_w[:], h_s[FIRST][:, chunk[3]], h_first[1][:, CHUNK:].rearrange("p j t -> p (j t)"))
+        last_half((2, 3))
+        for nt in range(NT):
+            y = ps.tile([P, JH], F32, name="y1_%d" % nt, tag="bank%d_%d" % (LAST, nt))
+            en4_pass(y[:, 0:CHUNK], nt, early_w[:, chunk[2]], chunk[2], start=True)
+            en4_pass(y[:, CHUNK:], nt, late_w[:], chunk[3], start=False)
+            if nt == 0:
+                en8_pass(y[:, 0:CHUNK], nt, chunk[2], stop=False)
+                en8_pass(y[:, CHUNK:], nt, chunk[3], stop=True)
+            else:
+                en8_pass(y[:], nt, half, stop=True)
+            finish(y[:], nt, half)

@@ -26,6 +26,9 @@ NT = N // P
 JH = J // 2
 
 FIRST, LAST = 1, 0
+TAIL = 192
+WB_PIECES = {(FIRST, 0): (0, PIECE), (FIRST, 1): (PIECE, PIECE), (LAST, 0): (0, PASS - TAIL), (LAST, 1): (PASS - TAIL, TAIL)}
+TM = (PASS - TAIL) // PACK
 TAB_ROW, TAB2_ROW = 12, 8
 WA_ROW = 4
 EN8_ROW, EN4_ROW = 4, 0
@@ -55,7 +58,7 @@ def tile_list_kg_relu_mix_sig_kernel(
         en4_w = tile("en4_w", [P, 2 * N], U8)
         en8_s = tile("en8_s", [P, N], U8)
         en4_s = tile("en4_s", [P, N], U8)
-        wb_raw = {(b, n): tile("wb_raw%d_%d" % (b, n), [P, PACK, PIECE], F32) for b in (FIRST, LAST) for n in range(2)}
+        wb_raw = {key: tile("wb_raw%d_%d" % key, [P, PACK, width], F32) for key, (first, width) in WB_PIECES.items()}
         warm_in = tile("warm_in", [P, 1], F32)
         warm_out = tile("warm_out", [P, 1], F32)
 
@@ -72,9 +75,9 @@ def tile_list_kg_relu_mix_sig_kernel(
                 eng.dma_start(dst[row + r : P : 32, :].bitcast(I32), src[0, r:16:4, :].bitcast(I32))
 
         def load_wb(b, n):
-            first = b * PASS + n * PIECE
+            first, width = WB_PIECES[b, n]
             rows = wb.rearrange("(p i) r -> p i r", i=PACK)
-            nc.sync.dma_start(wb_raw[b, n][:], rows[:, :, first : first + PIECE])
+            nc.sync.dma_start(wb_raw[b, n][:], rows[:, :, b * PASS + first : b * PASS + first + width])
 
         load_words(tab2_w, tab2_words)
         nc.sync.dma_start(idx2[:], offs2)
@@ -172,9 +175,9 @@ def tile_list_kg_relu_mix_sig_kernel(
         wa_passes(LAST, (0, 1))
         wa_passes(FIRST, (2, 3))
         wa_passes(LAST, (2,))
-        round_wb(wb_bf[LAST][:, :, 0:PM], raw[LAST, 0], nc.vector.tensor_copy)
+        round_wb(wb_bf[LAST][:, :, 0:TM], raw[LAST, 0], nc.vector.tensor_copy)
         for t in (0, 2):
-            round_wb(wb_bf[LAST][:, t : t + 2, PM:P], raw[LAST, 1][:, :, :, t : t + 2], nc.vector.tensor_copy)
+            round_wb(wb_bf[LAST][:, t : t + 2, TM:P], raw[LAST, 1][:, :, :, t : t + 2], nc.vector.tensor_copy)
         quantise_wb(LAST, 1)
         wb_passes(LAST, range(CHUNKS))
         wa_passes(LAST, (3,))
@@ -189,10 +192,12 @@ def tile_list_kg_relu_mix_sig_kernel(
         quantise(early_w[:, 0:JH], h_s[FIRST][:, 0:JH], h_first[0][:].rearrange("p j t -> p (j t)"))
         quantise(early_w[:, JH:], h_s[FIRST][:, JH : JH + CHUNK], h_first[1][:, 0:CHUNK].rearrange("p j t -> p (j t)"))
 
-        def last_half(chunks):
+        def last_relus(chunks):
             for c in chunks:
-                h_last[c] = tile("h_last%d" % c, [P, CHUNK, PACK], BF16, slot="h_last%d" % (1 if c == 3 else c))
+                h_last[c] = tile("h_last%d" % c, [P, CHUNK, PACK], BF16, slot="h_last%d" % (0 if c == 3 else c))
                 relu(h_last[c][:], LAST, c, on_scalar=(c % 2 == 0))
+
+        def last_quantise(chunks):
             for c in chunks:
                 js = slice(c * CHUNK, (c + 1) * CHUNK)
                 quantise(h_w[LAST][:, js], h_s[LAST][:, js], h_last[c][:].rearrange("p j t -> p (j t)"))
@@ -218,30 +223,37 @@ def tile_list_kg_relu_mix_sig_kernel(
 
         chunk = [slice(c * CHUNK, (c + 1) * CHUNK) for c in range(CHUNKS)]
         half = slice(0, JH)
-        last_half((0, 1))
-        y = [ps.tile([P, JH], F32, name="y0_%d" % nt, tag="bank%d_%d" % (FIRST, nt)) for nt in range(NT)]
-        for nt in range(2):
-            en4_pass(y[nt][:], nt, early_w[:, half], half, start=True)
-        for nt in range(NT):
-            if nt >= 2:
-                en4_pass(y[nt][:], nt, early_w[:, half], half, start=True)
-            if nt == 0:
-                en8_pass(y[nt][:, chunk[0]], nt, chunk[0], stop=False)
-                en8_pass(y[nt][:, chunk[1]], nt, chunk[1], stop=True)
-            else:
-                en8_pass(y[nt][:], nt, half, stop=True)
-            finish(y[nt][:], nt, half)
+        last_relus((0, 1))
+        last_quantise((0, 1))
+        lead = [ps.tile([P, 2, CHUNK], F32, name="lead%d" % c, tag="bank%d_%d" % (FIRST, c)) for c in range(2)]
+        for c in range(2):
+            for nt in range(2):
+                en4_pass(lead[c][:, nt, :], nt, early_w[:, chunk[c]], chunk[c], start=(nt == 0))
+        for c in range(2):
+            for nt in range(2):
+                en8_pass(lead[c][:, nt, :], nt, chunk[c], stop=(nt == 1))
+            lead_res = tile("lead_res%d" % c, [P, 2, CHUNK], F32)
+            nc.scalar.activation(lead_res[:], lead[c][:], ACT.Sigmoid)
+            nc.sync.dma_start(out_rows[:, 0:2, chunk[c]], lead_res[:])
+        for nt in (2, 3):
+            y = ps.tile([P, JH], F32, name="y0_%d" % nt, tag="bank%d_%d" % (FIRST, nt))
+            en4_pass(y[:], nt, early_w[:, half], half, start=True)
+            en8_pass(y[:], nt, half, stop=True)
+            finish(y[:], nt, half)
 
         half = slice(JH, J)
-        late_w = tile("late_w", [P, CHUNK], U32, slot="h_last0")
+        last_relus((2, 3))
+        last_quantise((2,))
+        late_w = tile("late_w", [P, CHUNK], U32, slot="h_last1")
         quantise(late_w[:], h_s[FIRST][:, chunk[3]], h_first[1][:, CHUNK:].rearrange("p j t -> p (j t)"))
-        last_half((2, 3))
+        last_quantise((3,))
         for nt in range(NT):
             y = ps.tile([P, JH], F32, name="y1_%d" % nt, tag="bank%d_%d" % (LAST, nt))
             en4_pass(y[:, 0:CHUNK], nt, early_w[:, chunk[2]], chunk[2], start=True)
-            en4_pass(y[:, CHUNK:], nt, late_w[:], chunk[3], start=False)
             if nt == 0:
                 en8_pass(y[:, 0:CHUNK], nt, chunk[2], stop=False)
+            en4_pass(y[:, CHUNK:], nt, late_w[:], chunk[3], start=False)
+            if nt == 0:
                 en8_pass(y[:, CHUNK:], nt, chunk[3], stop=True)
             else:
                 en8_pass(y[:], nt, half, stop=True)

from contextlib import ExitStack

import concourse.mybir as mybir

K, L, R, N, T, J = 512, 512, 1024, 512, 1024, 512
FLOPS = 2 * (K + L) * R * J + 2 * R * N * J

F32 = mybir.dt.float32
BF16 = mybir.dt.bfloat16
I32 = mybir.dt.int32
U32 = mybir.dt.uint32
U16 = mybir.dt.uint16
U8 = mybir.dt.uint8
FP8X4 = mybir.dt.float8_e4m3fn_x4
FP4X4 = mybir.dt.float4_e2m1fn_x4
ACT = mybir.ActivationFunctionType

P = 128
PACK = 4
PASS = P * PACK
CHUNK = 128
CHUNKS = J // CHUNK
PIECE = PASS // 2
PM = PIECE // PACK
NT = N // P
JH = J // 2

FIRST, LAST = 1, 0
TAIL = 192
WB_PIECES = {(FIRST, 0): (0, PIECE), (FIRST, 1): (PIECE, PIECE), (LAST, 0): (0, PASS - TAIL), (LAST, 1): (PASS - TAIL, TAIL)}
TM = (PASS - TAIL) // PACK
TAB_ROW, TAB2_ROW = 12, 8
WA_ROW = 4
EN8_ROW, EN4_ROW = 4, 0


def tile_list_kg_relu_mix_sig_kernel(
    tc, tab_words, tab_scales, tab2_words, tab2_scales, wa_words, wa_scales, wb,
    en8_words, en8_scales, en4_words, en4_scales, offs, offs2, out,
):
    nc = tc.nc
    with ExitStack() as ctx:
        sb = ctx.enter_context(tc.tile_pool(name="sb", bufs=1))
        ps = ctx.enter_context(tc.psum_pool(name="ps", bufs=1))

        def tile(name, shape, dtype, slot=None):
            return sb.tile(shape, dtype, name=name, tag=slot or name, align_bytes=64)

        idx = tile("idx", [P, J // 16], U16)
        idx2 = tile("idx2", [P, J // 16], U16)
        tab_w = tile("tab_w", [P, T], I32)
        tab_s = tile("tab_s", [P, T], U8)
        tab2_w = tile("tab2_w", [P, T], I32)
        tab2_s = tile("tab2_s", [P, T], U8)
        wa_w = tile("wa_w", [P, R], I32)
        wa_s = tile("wa_s", [P, R], U8)
        en8_w = tile("en8_w", [P, N], I32)
        en4_w = tile("en4_w", [P, 2 * N], U8)
        en8_s = tile("en8_s", [P, N], U8)
        en4_s = tile("en4_s", [P, N], U8)
        wb_raw = {key: tile("wb_raw%d_%d" % key, [P, PACK, width], F32) for key, (first, width) in WB_PIECES.items()}
        warm_in = tile("warm_in", [P, 1], F32)
        warm_out = tile("warm_out", [P, 1], F32)

        for plane in (tab2_s, wa_s, tab_s, en4_s, en8_s):
            nc.vector.memset(plane[:].bitcast(I32), 0)
        nc.vector.memset(warm_in[:], 0.0)
        nc.scalar.activation(warm_out[:], warm_in[:], ACT.Sigmoid)

        def load_words(dst, src):
            nc.sync.dma_start(dst[:], src[0].rearrange("p n i -> p (n i)").bitcast(I32))

        def load_scales(dst, row, src, eng):
            for r in range(4):
                eng.dma_start(dst[row + r : P : 32, :].bitcast(I32), src[0, r:16:4, :].bitcast(I32))

        def load_wb(b, n):
            first, width = WB_PIECES[b, n]
            rows = wb.rearrange("(p i) r -> p i r", i=PACK)
            nc.sync.dma_start(wb_raw[b, n][:], rows[:, :, b * PASS + first : b * PASS + first + width])

        load_words(tab2_w, tab2_words)
        nc.sync.dma_start(idx2[:], offs2)
        load_scales(tab2_s, TAB2_ROW, tab2_scales, nc.sync)
        load_wb(FIRST, 0)
        load_wb(FIRST, 1)
        nc.sync.dma_start(idx[:], offs)
        load_scales(wa_s, WA_ROW, wa_scales, nc.sync)
        load_words(tab_w, tab_words)
        load_words(wa_w, wa_words)
        load_scales(tab_s, TAB_ROW, tab_scales, nc.sync)
        load_wb(LAST, 0)
        load_wb(LAST, 1)
        load_scales(en8_s, EN8_ROW, en8_scales, nc.sync)
        load_words(en8_w, en8_words)
        nc.sync.dma_start(en4_w[:].bitcast(I32), en4_words[0].bitcast(I32))
        load_scales(en4_s, EN4_ROW, en4_scales, nc.sync)

        v_s = tile("v_s", [P, J], U8)
        v_w = tile("v_w", [P, J], U32)
        wa_pw = {b: tile("wa_pw%d" % b, [P, PASS], U32) for b in (FIRST, LAST)}
        v2_w = tile("v2_w", [P, J], U32)
        v2_s = tile("v2_s", [P, J], U8)
        wb_w = {b: tile("wb_w%d" % b, [P, PASS], U32) for b in (FIRST, LAST)}
        wb_s = {b: tile("wb_s%d" % b, [P, PASS], U8) for b in (FIRST, LAST)}
        h_s = {b: tile("h_s%d" % b, [P, J], U8) for b in (FIRST, LAST)}
        h_w = {LAST: tile("h_w%d" % LAST, [P, J], U32)}
        z = {(b, c): ps.tile([P, PACK, CHUNK], F32, name="z%d_%d" % (b, c), tag="bank%d_%d" % (b, c)) for b in (FIRST, LAST) for c in range(CHUNKS)}

        def deal_wa_words(b):
            nc.scalar.copy(
                wa_pw[b][:].rearrange("p (t g m) -> p g t m", t=PACK, m=4),
                wa_w[:, b * PASS : (b + 1) * PASS].bitcast(U32).rearrange("p (g m t) -> p g t m", t=PACK, m=4),
            )

        def round_wb(dst, raw, copy):
            copy(dst.rearrange("p t m i -> p m i t"), raw.rearrange("p i m t -> p m i t"))

        def quantise(words, scales, values):
            nc.vector.quantize_mx(out=words.bitcast(FP8X4), scales=scales, in_=values)

        def quantise_wb(b, tiles):
            for t in range(0, PACK, tiles):
                cols = slice(t * P, (t + tiles) * P)
                quantise(wb_w[b][:, cols], wb_s[b][:, cols], wb_bf[b][:, t : t + tiles].rearrange("p t m i -> p (t m i)"))

        def z_passes(b, c, lhs_w, lhs_s, rhs_w, rhs_s, first):
            order = range(PACK) if b == FIRST or c < 2 else range(PACK - 1, -1, -1)
            for t in order:
                cols = slice(t * P, (t + 1) * P)
                nc.tensor.matmul_mx(
                    out=z[b, c][:, t, :], lhsT=lhs_w[:, cols].bitcast(FP8X4), lhsT_scale=lhs_s[:, cols],
                    rhs=rhs_w.bitcast(FP8X4), rhs_scale=rhs_s,
                    start=(first and t == order[0]), stop=(not first and t == order[-1]),
                )

        def wa_passes(b, chunks):
            for c in chunks:
                js = slice(c * CHUNK, (c + 1) * CHUNK)
                z_passes(b, c, wa_pw[b][:], wa_ps[WA_ROW:, b * PASS : (b + 1) * PASS], v_w[:, js], v_s[TAB_ROW:, js], first=(b == LAST and c < CHUNKS - 1))

        def wb_passes(b, chunks):
            for c in chunks:
                js = slice(c * CHUNK, (c + 1) * CHUNK)
                z_passes(b, c, wb_w[b][:], wb_s[b][:], v2_w[:, js], v2_s[TAB2_ROW:, js], first=(b == FIRST or c == CHUNKS - 1))

        def relu(dst, b, c, on_scalar):
            src = z[b, c][:].rearrange("p t j -> p j t")
            if on_scalar:
                nc.scalar.activation(dst, src, ACT.Relu)
            else:
                nc.vector.tensor_scalar_max(dst, src, 0.0)

        raw = {key: r[:].rearrange("p i (m t) -> p i m t", t=PACK) for key, r in wb_raw.items()}
        wb_bf = {b: tile("wb_bf%d" % b, [P, PACK, P, PACK], BF16) for b in (FIRST, LAST)}
        nc.vector.tensor_copy(v2_w[:], tab2_w[:].bitcast(U32).indirect(idx2[:]))
        nc.vector.tensor_copy(v2_s[:], tab2_s[:].indirect(idx2[:]))
        round_wb(wb_bf[FIRST][:, :, 0:PM], raw[FIRST, 0], nc.scalar.copy)
        round_wb(wb_bf[FIRST][:, 2:4, PM:P], raw[FIRST, 1][:, :, :, 2:4], nc.scalar.copy)
        round_wb(wb_bf[FIRST][:, 0:2, PM:P], raw[FIRST, 1][:, :, :, 0:2], nc.vector.tensor_copy)
        quantise_wb(FIRST, 1)
        wb_passes(FIRST, range(CHUNKS))
        wa_ps = tile("wa_ps", [P, R], U8, slot="wb_bf%d" % FIRST)
        nc.vector.tensor_copy(v_w[:], tab_w[:].bitcast(U32).indirect(idx[:]))
        for first, last in ((0, CHUNK), (CHUNK, JH), (JH, J)):
            nc.vector.tensor_copy(v_s[:, first:last], tab_s[:].indirect(idx[:, first // 16 : last // 16]))
        for b in (FIRST, LAST):
            half = slice(b * PASS, (b + 1) * PASS)
            deal_wa_words(b)
            nc.gpsimd.tensor_copy(
                wa_ps[:, half].rearrange("p (t m) -> p t m", t=PACK),
                wa_s[:, half].rearrange("p (m t) -> p t m", t=PACK),
            )
        wa_passes(FIRST, (0, 1))
        wa_passes(LAST, (0, 1))
        wa_passes(FIRST, (2, 3))
        wa_passes(LAST, (2,))
        round_wb(wb_bf[LAST][:, :, 0:TM], raw[LAST, 0], nc.vector.tensor_copy)
        for t in (0, 2):
            round_wb(wb_bf[LAST][:, t : t + 2, TM:P], raw[LAST, 1][:, :, :, t : t + 2], nc.vector.tensor_copy)
        quantise_wb(LAST, 1)
        wb_passes(LAST, range(CHUNKS))
        wa_passes(LAST, (3,))

        h_first = [tile("h_first%d" % jh, [P, JH, PACK], BF16) for jh in range(2)]
        h_last = {}
        for c in range(CHUNKS):
            relu(h_first[c // 2][:, c % 2 * CHUNK : (c % 2 + 1) * CHUNK, :], FIRST, c, on_scalar=True)

        out_rows = out.rearrange("(nt p) j -> p nt j", p=P)
        early_w = tile("early_w", [P, JH + CHUNK], U32, slot="wb_raw%d_1" % LAST)
        quantise(early_w[:, 0:JH], h_s[FIRST][:, 0:JH], h_first[0][:].rearrange("p j t -> p (j t)"))
        quantise(early_w[:, JH:], h_s[FIRST][:, JH : JH + CHUNK], h_first[1][:, 0:CHUNK].rearrange("p j t -> p (j t)"))

        def last_relus(chunks):
            for c in chunks:
                h_last[c] = tile("h_last%d" % c, [P, CHUNK, PACK], BF16, slot="h_last%d" % (0 if c == 3 else c))
                relu(h_last[c][:], LAST, c, on_scalar=(c % 2 == 0))

        def last_quantise(chunks):
            for c in chunks:
                js = slice(c * CHUNK, (c + 1) * CHUNK)
                quantise(h_w[LAST][:, js], h_s[LAST][:, js], h_last[c][:].rearrange("p j t -> p (j t)"))

        def en4_pass(dst, nt, words, js, start):
            nc.tensor.matmul_mx(
                out=dst, lhsT=en4_w[:, 2 * nt * P : 2 * (nt + 1) * P].bitcast(FP4X4),
                lhsT_scale=en4_s[EN4_ROW:, nt * P : (nt + 1) * P],
                rhs=words.bitcast(FP8X4), rhs_scale=h_s[FIRST][:, js], start=start, stop=False,
            )

        def en8_pass(dst, nt, js, stop):
            cols = slice(nt * P, (nt + 1) * P)
            nc.tensor.matmul_mx(
                out=dst, lhsT=en8_w[:, cols].bitcast(FP8X4), lhsT_scale=en8_s[EN8_ROW:, cols],
                rhs=h_w[LAST][:, js].bitcast(FP8X4), rhs_scale=h_s[LAST][:, js], start=False, stop=stop,
            )

        def finish(src, nt, half):
            res = tile("res%d_%d" % (half.start, nt), [P, JH], F32)
            nc.scalar.activation(res[:], src, ACT.Sigmoid)
            nc.sync.dma_start(out_rows[:, nt, half], res[:])

        chunk = [slice(c * CHUNK, (c + 1) * CHUNK) for c in range(CHUNKS)]
        half = slice(0, JH)
        last_relus((0, 1))
        last_quantise((0, 1))
        lead = [ps.tile([P, 2, CHUNK], F32, name="lead%d" % c, tag="bank%d_%d" % (FIRST, c)) for c in range(2)]
        for c in range(2):
            for nt in range(2):
                en4_pass(lead[c][:, nt, :], nt, early_w[:, chunk[c]], chunk[c], start=(nt == 0))
        for c in range(2):
            for nt in range(2):
                en8_pass(lead[c][:, nt, :], nt, chunk[c], stop=(nt == 1))
            lead_res = tile("lead_res%d" % c, [P, 2, CHUNK], F32)
            nc.scalar.activation(lead_res[:], lead[c][:], ACT.Sigmoid)
            nc.sync.dma_start(out_rows[:, 0:2, chunk[c]], lead_res[:])
        for nt in (2, 3):
            y = ps.tile([P, JH], F32, name="y0_%d" % nt, tag="bank%d_%d" % (FIRST, nt))
            en4_pass(y[:], nt, early_w[:, half], half, start=True)
            en8_pass(y[:], nt, half, stop=True)
            finish(y[:], nt, half)

        half = slice(JH, J)
        last_relus((2, 3))
        last_quantise((2,))
        late_w = tile("late_w", [P, CHUNK], U32, slot="h_last1")
        quantise(late_w[:], h_s[FIRST][:, chunk[3]], h_first[1][:, CHUNK:].rearrange("p j t -> p (j t)"))
        last_quantise((3,))
        for nt in range(NT):
            y = ps.tile([P, JH], F32, name="y1_%d" % nt, tag="bank%d_%d" % (LAST, nt))
            en4_pass(y[:, 0:CHUNK], nt, early_w[:, chunk[2]], chunk[2], start=True)
            if nt == 0:
                en8_pass(y[:, 0:CHUNK], nt, chunk[2], stop=False)
            en4_pass(y[:, CHUNK:], nt, late_w[:], chunk[3], start=False)
            if nt == 0:
                en8_pass(y[:, CHUNK:], nt, chunk[3], stop=True)
            else:
                en8_pass(y[:], nt, half, stop=True)
            finish(y[:], nt, half)
